import numpy as np
import ml_dtypes


def mxq(x, axis, fmt="e4m3"):
    dtype, down = {"e4m3": (ml_dtypes.float8_e4m3fn, 7), "e5m2": (ml_dtypes.float8_e5m2, 14)}[fmt]
    v = np.moveaxis(np.asarray(x, np.float32).astype(ml_dtypes.bfloat16).astype(np.float64), axis, -1)
    blocks = v.reshape(v.shape[:-1] + (-1, 32))
    amax = np.abs(blocks).max(-1, keepdims=True)
    byte = np.maximum(np.where(amax > 0, np.frexp(amax)[1] - 1 + 127, 0) - down, 1)
    scale = np.exp2(byte - 127.0)
    codes = (blocks / scale).astype(np.float32).astype(dtype).astype(np.float64)
    return np.moveaxis((codes * scale).reshape(v.shape), -1, axis)


WIDE = False


def mx_kscale(k):
    if not WIDE:
        return np.ones(k)
    levels = np.array([18, -18])
    if k % 512:
        return np.exp2(np.random.permutation(np.resize(levels, k // 32))).repeat(32)
    a = np.empty((k // 512, 16))
    for p in range(k // 512):
        a[p, :8] = np.random.permutation(np.resize(levels, 8))
        for g in range(8):
            far = levels[np.abs(levels - a[p, g]) >= 10]
            a[p, g + 8] = far[np.random.randint(len(far))]
    return np.exp2(a.ravel()).repeat(32)


def f64(x):
    return np.asarray(x).astype(np.float64)


def striped(idx):
    return np.tile(np.asarray(idx).reshape(-1, 16).T, (8, 1)).astype(np.uint16)


def unstriped(offs):
    return offs[:16].T.reshape(-1).astype(np.int64)

def planes(y):
    n, m = y.shape
    v = y.astype(np.float32).astype(ml_dtypes.bfloat16).astype(np.float64).reshape(n // 32, 32, m)
    top = np.abs(v).max(1)
    byte = np.clip(np.where(top > 0, np.frexp(top)[1] - 1 + 127 - 7, 1), 1, 254)
    codes = (v * np.exp2(127.0 - byte)[:, None, :]).reshape(n, m).astype(np.float32).astype(ml_dtypes.float8_e4m3fn).view(np.uint8)
    words = codes.reshape(n // 512, 128, 4, m).transpose(0, 1, 3, 2)
    return np.ascontiguousarray(words), np.ascontiguousarray(byte.astype(np.uint8).reshape(n // 512, 16, m))


def setup_inputs():
    n = np.random.standard_normal
    uni = np.random.uniform
    idx = np.random.permutation(2048)[:512]
    f_i = np.ones(2048)
    f_i[idx] = mx_kscale(512)
    return {
        "dy": (n((512, 2048)) * f_i[None, :]).astype(np.float32),
        "wT": (n((512, 2048)) / np.sqrt(512) / f_i[None, :]).astype(np.float32),
        "offs": striped(idx),
    }


def reference(dy, wT, offs):
    idx = unstriped(offs)
    dy_ = f64(dy)[:, idx]
    wT_i = f64(wT)[:, idx]
    out_0 = mxq(wT_i, 1, "e4m3") @ mxq(dy_, 1, "e5m2").T
    return (out_0,) + planes(out_0)

@@ -1,0 +1,135 @@
+from contextlib import ExitStack
+
+import concourse.mybir as mybir
+from concourse.masks import make_identity
+
+F32 = mybir.dt.float32
+BF16 = mybir.dt.bfloat16
+I32 = mybir.dt.int32
+U32 = mybir.dt.uint32
+U16 = mybir.dt.uint16
+U8 = mybir.dt.uint8
+E4M3X4 = mybir.dt.float8_e4m3fn_x4
+E5M2X4 = mybir.dt.float8_e5m2_x4
+
+P = 128
+LANES = 4
+D = 512
+R = 512
+SLOTS = 512
+UNITS = 2048
+TAIL_CHUNKS = 4
+
+FLOPS = 2 * D * R * SLOTS
+
+
+def tile_attend_gmeprop_x_pl_kernel(tc, dy, wT, offs, out_0, out_1, out_2):
+    nc = tc.nc
+    w_rows = wT.rearrange("(p t) k -> p t k", t=LANES)
+    out_rows = out_0.rearrange("(p t) r -> p t r", t=LANES)
+    out_words = out_1.rearrange("a p c l -> (a p) (c l)").bitcast(I32)
+    out_scales = out_2.rearrange("a q c -> (a q) c").bitcast(I32)
+
+    with ExitStack() as ctx:
+        keep = ctx.enter_context(tc.tile_pool(name="keep", bufs=1))
+        ring = ctx.enter_context(tc.tile_pool(name="ring", bufs=2))
+        turn = ctx.enter_context(tc.psum_pool(name="turn", bufs=2))
+        sums = ctx.enter_context(tc.psum_pool(name="sums", bufs=1))
+
+        offsets = keep.tile([P, SLOTS // 16], U16, name="offsets")
+        windows = []
+        for n in range(2 * LANES):
+            window = keep.tile([P, UNITS], F32, name="window%d" % n, tag="window%d" % n, align_bytes=64)
+            source = dy[n * P : (n + 1) * P, :] if n < LANES else w_rows[:, n - LANES, :]
+            nc.sync.dma_start(out=window[:], in_=source)
+            if n == 0:
+                nc.sync.dma_start(offsets[:], offs)
+            windows.append(window)
+
+        identity = keep.tile([P, P], F32, name="identity")
+        make_identity(nc, identity[:])
+
+        def gather(window):
+            picked = ring.tile([P, SLOTS], BF16, name="picked", align_bytes=64)
+            nc.vector.tensor_copy(picked[:], window[:].indirect(offsets[:]))
+            return picked
+
+        def turn_slots_onto_partitions(picked, grouped):
+            pairs = picked[:].bitcast(F32)
+            turned = turn.tile([P, 2, P], F32, name="turned")
+            for u in range(2):
+                nc.tensor.transpose(turned[:, u, :], pairs[:, u : 2 * P : 2], identity[:])
+            nc.scalar.copy(
+                out=grouped.bitcast(F32).rearrange("p (m u) -> p m u", u=2),
+                in_=turned[:].rearrange("p u m -> p m u"),
+            )
+
+        dy_grouped = keep.tile([P, LANES * R], BF16, name="dy_grouped", align_bytes=64)
+        for q in range(LANES):
+            turn_slots_onto_partitions(gather(windows[q]), dy_grouped[:, q * LANES * P : (q + 1) * LANES * P])
+
+        w_grouped = [
+            keep.tile([P, LANES * P], BF16, name="w_grouped%d" % t, tag="w_grouped%d" % t, align_bytes=64)
+            for t in range(LANES)
+        ]
+        turn_slots_onto_partitions(gather(windows[LANES]), w_grouped[0][:])
+        dy_codes = keep.tile([P, R], U32, name="dy_codes", tag="window%d" % LANES, align_bytes=64)
+        dy_scales = keep.tile([P, R], U8, name="dy_scales", align_bytes=64)
+        nc.vector.quantize_mx(out=dy_codes[:].bitcast(E5M2X4), scales=dy_scales[:], in_=dy_grouped[:])
+
+        y = keep.tile([P, LANES, R], F32, name="y", align_bytes=64)
+        y_codes = keep.tile([P, R], U32, name="y_codes", align_bytes=64)
+        y_scales = keep.tile([P, R], U8, name="y_scales", align_bytes=64)
+        last = LANES - 1
+        for t in range(LANES):
+            if t < last:
+                turn_slots_onto_partitions(gather(windows[LANES + t + 1]), w_grouped[t + 1][:])
+                codes_tag = "window%d" % (LANES + t + 1)
+            else:
+                codes_tag = "w_codes_last"
+            w_codes = keep.tile([P, P], U32, name="w_codes%d" % t, tag=codes_tag, align_bytes=64)
+            w_scales = keep.tile([P, P], U8, name="w_scales%d" % t, align_bytes=64)
+            nc.vector.quantize_mx(out=w_codes[:].bitcast(E4M3X4), scales=w_scales[:], in_=w_grouped[t][:])
+            if t == last - 1:
+                y_grouped = keep.tile([P, R, LANES], BF16, name="y_grouped", tag="w_grouped%d" % t, align_bytes=64)
+                nc.vector.tensor_copy(out=y_grouped[:, :, 0:2], in_=y[:, 0:2, :].rearrange("p t r -> p r t"))
+            bank = sums.tile([P, R], F32, name="bank%d" % t)
+            nc.tensor.matmul_mx(
+                out=bank[:],
+                lhsT=w_codes[:].bitcast(E4M3X4),
+                lhsT_scale=w_scales[:],
+                rhs=dy_codes[:].bitcast(E5M2X4),
+                rhs_scale=dy_scales[:],
+                start=True,
+                stop=True,
+            )
+            if t < last:
+                nc.scalar.copy(out=y[:, t, :], in_=bank[:])
+                nc.sync.dma_start(out=out_rows[:, t, :], in_=y[:, t, :])
+
+        width = R // TAIL_CHUNKS
+        chunks = [slice(c * width, (c + 1) * width) for c in range(TAIL_CHUNKS)]
+
+        def quantize_result(cols):
+            nc.vector.quantize_mx(
+                out=y_codes[:, cols].bitcast(E4M3X4),
+                scales=y_scales[:, cols],
+                in_=y_grouped[:, cols, :].rearrange("p r t -> p (r t)"),
+            )
+
+        for c, cols in enumerate(chunks):
+            nc.scalar.copy(out=y[:, last, cols], in_=bank[:, cols])
+            nc.vector.tensor_copy(out=y_grouped[:, cols, 2:4], in_=y[:, 2:4, cols].rearrange("p t r -> p r t"))
+            if c > 0:
+                quantize_result(chunks[c - 1])
+        nc.sync.dma_start(out=out_rows[:, last, :], in_=y[:, last, :])
+        half = R // 2
+        nc.sync.dma_start(out=out_words[:, 0:half], in_=y_codes[:, 0:half].bitcast(I32))
+        quantize_result(chunks[-1])
+        nc.sync.dma_start(out=out_words[:, half:R], in_=y_codes[:, half:R].bitcast(I32))
+        for quad in range(4):
+            queue = nc.scalar if quad % 2 == 0 else nc.sync
+            queue.dma_start(
+                out=out_scales[4 * quad : 4 * quad + 4, :],
+                in_=y_scales[32 * quad : 32 * quad + 4, :].bitcast(I32),
+            )

@@ -37,75 +37,108 @@ def tile_attend_gmeprop_x_pl_kernel(tc, dy, wT, offs, out_0, out_1, out_2):
         sums = ctx.enter_context(tc.psum_pool(name="sums", bufs=1))
 
         offsets = keep.tile([P, SLOTS // 16], U16, name="offsets")
-        windows = []
-        for n in range(2 * LANES):
-            window = keep.tile([P, UNITS], F32, name="window%d" % n, tag="window%d" % n, align_bytes=64)
-            source = dy[n * P : (n + 1) * P, :] if n < LANES else w_rows[:, n - LANES, :]
-            nc.sync.dma_start(out=window[:], in_=source)
-            if n == 0:
+        dy_rows = dy.rearrange("(q p j) k -> q p j k", p=P, j=2)
+        dy_tiles = []
+        for q in range(2):
+            dy_tile = keep.tile([P, 2, UNITS], F32, name="dy_tile%d" % q, align_bytes=64)
+            nc.sync.dma_start(out=dy_tile[:], in_=dy_rows[q])
+            if q == 0:
                 nc.sync.dma_start(offsets[:], offs)
-            windows.append(window)
+            dy_tiles.append(dy_tile)
+        w_first = []
+        for t in range(2):
+            w_tile = keep.tile([P, UNITS], F32, name="w_tile%d" % t, tag="w_tile%d" % t, align_bytes=64)
+            nc.sync.dma_start(out=w_tile[:], in_=w_rows[:, t, :])
+            w_first.append(w_tile)
+        w_third = keep.tile([P, UNITS], F32, name="w_third", tag="w_third", align_bytes=64)
+        nc.sync.dma_start(out=w_third[:], in_=w_rows[:, 2, :])
+        w_last = keep.tile([P, UNITS], F32, name="w_last", tag="w_last", align_bytes=64)
+        nc.sync.dma_start(out=w_last[:], in_=w_rows[:, 3, :])
 
         identity = keep.tile([P, P], F32, name="identity")
         make_identity(nc, identity[:])
 
-        def gather(window):
-            picked = ring.tile([P, SLOTS], BF16, name="picked", align_bytes=64)
-            nc.vector.tensor_copy(picked[:], window[:].indirect(offsets[:]))
-            return picked
-
-        def turn_slots_onto_partitions(picked, grouped):
-            pairs = picked[:].bitcast(F32)
-            turned = turn.tile([P, 2, P], F32, name="turned")
-            for u in range(2):
-                nc.tensor.transpose(turned[:, u, :], pairs[:, u : 2 * P : 2], identity[:])
-            nc.scalar.copy(
-                out=grouped.bitcast(F32).rearrange("p (m u) -> p m u", u=2),
-                in_=turned[:].rearrange("p u m -> p m u"),
+        def gather_and_turn(window, turned, picked=None):
+            if picked is None:
+                picked = ring.tile([P, SLOTS], BF16, name="picked", align_bytes=64)
+            nc.vector.tensor_copy(
+                picked[:].rearrange("p (h b e) -> p b h e", h=2, e=16), window.indirect(offsets[:])
             )
+            pairs = picked[:].bitcast(F32)
+            for h in range(2):
+                nc.tensor.transpose(turned[:, h, :], pairs[:, h * P : (h + 1) * P], identity[:])
 
         dy_grouped = keep.tile([P, LANES * R], BF16, name="dy_grouped", align_bytes=64)
-        for q in range(LANES):
-            turn_slots_onto_partitions(gather(windows[q]), dy_grouped[:, q * LANES * P : (q + 1) * LANES * P])
+        for q in range(2):
+            turned = turn.tile([P, 2, 2, P], F32, name="turned")
+            for j in range(2):
+                gather_and_turn(dy_tiles[q][:, j, :], turned[:, j])
+            nc.scalar.copy(
+                out=dy_grouped[:, q * 2 * R : (q + 1) * 2 * R].bitcast(F32).rearrange("p (m j h) -> p m j h", j=2, h=2),
+                in_=turned[:].rearrange("p j h m -> p m j h"),
+            )
 
-        w_grouped = [
-            keep.tile([P, LANES * P], BF16, name="w_grouped%d" % t, tag="w_grouped%d" % t, align_bytes=64)
-            for t in range(LANES)
-        ]
-        turn_slots_onto_partitions(gather(windows[LANES]), w_grouped[0][:])
-        dy_codes = keep.tile([P, R], U32, name="dy_codes", tag="window%d" % LANES, align_bytes=64)
-        dy_scales = keep.tile([P, R], U8, name="dy_scales", align_bytes=64)
-        nc.vector.quantize_mx(out=dy_codes[:].bitcast(E5M2X4), scales=dy_scales[:], in_=dy_grouped[:])
+        def prepare_w(window, grouped, picked=None, turned=None):
+            if turned is None:
+                turned = turn.tile([P, 2, P], F32, name="turned")
+            gather_and_turn(window, turned, picked)
+            nc.scalar.copy(
+                out=grouped.bitcast(F32).rearrange("p (m h) -> p m h", h=2),
+                in_=turned[:].rearrange("p h m -> p m h"),
+            )
 
-        y = keep.tile([P, LANES, R], F32, name="y", align_bytes=64)
-        y_codes = keep.tile([P, R], U32, name="y_codes", align_bytes=64)
-        y_scales = keep.tile([P, R], U8, name="y_scales", align_bytes=64)
-        last = LANES - 1
-        for t in range(LANES):
-            if t < last:
-                turn_slots_onto_partitions(gather(windows[LANES + t + 1]), w_grouped[t + 1][:])
-                codes_tag = "window%d" % (LANES + t + 1)
-            else:
-                codes_tag = "w_codes_last"
-            w_codes = keep.tile([P, P], U32, name="w_codes%d" % t, tag=codes_tag, align_bytes=64)
-            w_scales = keep.tile([P, P], U8, name="w_scales%d" % t, align_bytes=64)
-            nc.vector.quantize_mx(out=w_codes[:].bitcast(E4M3X4), scales=w_scales[:], in_=w_grouped[t][:])
-            if t == last - 1:
-                y_grouped = keep.tile([P, R, LANES], BF16, name="y_grouped", tag="w_grouped%d" % t, align_bytes=64)
-                nc.vector.tensor_copy(out=y_grouped[:, :, 0:2], in_=y[:, 0:2, :].rearrange("p t r -> p r t"))
-            bank = sums.tile([P, R], F32, name="bank%d" % t)
+        def quantize_w(grouped, name, codes_tag):
+            columns = grouped.shape[1] // LANES
+            codes = keep.tile([P, columns], U32, name=name + "_codes", tag=codes_tag, align_bytes=64)
+            scales = keep.tile([P, columns], U8, name=name + "_scales", align_bytes=64)
+            nc.vector.quantize_mx(out=codes[:].bitcast(E4M3X4), scales=scales[:], in_=grouped)
+            return codes, scales
+
+        def multiply(t, codes, scales):
+            bank = sums.tile([P, R], F32, name="bank%d" % t, tag="bank%d" % t)
             nc.tensor.matmul_mx(
                 out=bank[:],
-                lhsT=w_codes[:].bitcast(E4M3X4),
-                lhsT_scale=w_scales[:],
+                lhsT=codes.bitcast(E4M3X4),
+                lhsT_scale=scales,
                 rhs=dy_codes[:].bitcast(E5M2X4),
                 rhs_scale=dy_scales[:],
                 start=True,
                 stop=True,
             )
-            if t < last:
-                nc.scalar.copy(out=y[:, t, :], in_=bank[:])
-                nc.sync.dma_start(out=out_rows[:, t, :], in_=y[:, t, :])
+            return bank
+
+        y = keep.tile([P, LANES, R], F32, name="y", align_bytes=64)
+        y_codes = keep.tile([P, R], U32, name="y_codes", align_bytes=64)
+        y_scales = keep.tile([P, R], U8, name="y_scales", align_bytes=64)
+        last = LANES - 1
+
+        first_grouped = keep.tile([P, 2 * LANES * P], BF16, name="first_grouped", tag="first_grouped", align_bytes=64)
+        third_grouped = keep.tile([P, LANES * P], BF16, name="third_grouped", tag="third_grouped", align_bytes=64)
+        last_grouped = keep.tile([P, LANES * P], BF16, name="last_grouped", align_bytes=64)
+        prepare_w(w_first[0][:], first_grouped[:, 0 : LANES * P])
+        dy_codes = keep.tile([P, R], U32, name="dy_codes", tag="w_tile0", align_bytes=64)
+        dy_scales = keep.tile([P, R], U8, name="dy_scales", align_bytes=64)
+        nc.vector.quantize_mx(out=dy_codes[:].bitcast(E5M2X4), scales=dy_scales[:], in_=dy_grouped[:])
+        prepare_w(w_first[1][:], first_grouped[:, LANES * P : 2 * LANES * P])
+        prepare_w(w_third[:], third_grouped[:])
+        codes, scales = quantize_w(first_grouped[:], "first", "w_third")
+        for t in range(2):
+            bank = multiply(t, codes[:, t * P : (t + 1) * P], scales[:, t * P : (t + 1) * P])
+            nc.scalar.copy(out=y[:, t, :], in_=bank[:])
+        nc.sync.dma_start(out=out_rows[:, 0:2, :], in_=y[:, 0:2, :])
+
+        last_picked = keep.tile([P, SLOTS], BF16, name="last_picked", tag="first_grouped", align_bytes=64)
+        last_turned = sums.tile([P, 2, P], F32, name="last_turned", tag="bank0")
+        prepare_w(w_last[:], last_grouped[:], last_picked, last_turned)
+        codes, scales = quantize_w(third_grouped[:], "third", "w_last")
+        y_grouped = keep.tile([P, R, LANES], BF16, name="y_grouped", tag="third_grouped", align_bytes=64)
+        nc.vector.tensor_copy(out=y_grouped[:, :, 0:2], in_=y[:, 0:2, :].rearrange("p t r -> p r t"))
+        bank = multiply(2, codes[:], scales[:])
+        nc.scalar.copy(out=y[:, 2, :], in_=bank[:])
+        nc.sync.dma_start(out=out_rows[:, 2, :], in_=y[:, 2, :])
+
+        codes, scales = quantize_w(last_grouped[:], "last", "last_codes")
+        bank = multiply(last, codes[:], scales[:])
 
         width = R // TAIL_CHUNKS
         chunks = [slice(c * width, (c + 1) * width) for c in range(TAIL_CHUNKS)]
@@ -117,14 +150,16 @@ def tile_attend_gmeprop_x_pl_kernel(tc, dy, wT, offs, out_0, out_1, out_2):
                 in_=y_grouped[:, cols, :].rearrange("p r t -> p (r t)"),
             )
 
-        for c, cols in enumerate(chunks):
+        for cols in chunks:
             nc.scalar.copy(out=y[:, last, cols], in_=bank[:, cols])
-            nc.vector.tensor_copy(out=y_grouped[:, cols, 2:4], in_=y[:, 2:4, cols].rearrange("p t r -> p r t"))
-            if c > 0:
-                quantize_result(chunks[c - 1])
         nc.sync.dma_start(out=out_rows[:, last, :], in_=y[:, last, :])
+        for cols in chunks[:-1]:
+            nc.vector.tensor_copy(out=y_grouped[:, cols, 2:4], in_=y[:, 2:4, cols].rearrange("p t r -> p r t"))
+        nc.scalar.copy(out=y_grouped[:, chunks[-1], 2:4], in_=y[:, 2:4, chunks[-1]].rearrange("p t r -> p r t"))
         half = R // 2
+        quantize_result(slice(0, half))
         nc.sync.dma_start(out=out_words[:, 0:half], in_=y_codes[:, 0:half].bitcast(I32))
+        quantize_result(chunks[-2])
         quantize_result(chunks[-1])
         nc.sync.dma_start(out=out_words[:, half:R], in_=y_codes[:, half:R].bitcast(I32))
         for quad in range(4):

@@ -113,8 +113,8 @@ def tile_attend_gmeprop_x_pl_kernel(tc, dy, wT, offs, out_0, out_1, out_2):
         last = LANES - 1
 
         first_grouped = keep.tile([P, 2 * LANES * P], BF16, name="first_grouped", tag="first_grouped", align_bytes=64)
-        third_grouped = keep.tile([P, LANES * P], BF16, name="third_grouped", tag="third_grouped", align_bytes=64)
-        last_grouped = keep.tile([P, LANES * P], BF16, name="last_grouped", align_bytes=64)
+        third_grouped = keep.tile([P, LANES * P], BF16, name="third_grouped", align_bytes=64)
+        last_grouped = keep.tile([P, LANES * P], BF16, name="last_grouped", tag="last_grouped", align_bytes=64)
         prepare_w(w_first[0][:], first_grouped[:, 0 : LANES * P])
         dy_codes = keep.tile([P, R], U32, name="dy_codes", tag="w_tile0", align_bytes=64)
         dy_scales = keep.tile([P, R], U8, name="dy_scales", align_bytes=64)
@@ -131,13 +131,13 @@ def tile_attend_gmeprop_x_pl_kernel(tc, dy, wT, offs, out_0, out_1, out_2):
         last_turned = sums.tile([P, 2, P], F32, name="last_turned", tag="bank0")
         prepare_w(w_last[:], last_grouped[:], last_picked, last_turned)
         codes, scales = quantize_w(third_grouped[:], "third", "w_last")
-        y_grouped = keep.tile([P, R, LANES], BF16, name="y_grouped", tag="third_grouped", align_bytes=64)
-        nc.vector.tensor_copy(out=y_grouped[:, :, 0:2], in_=y[:, 0:2, :].rearrange("p t r -> p r t"))
         bank = multiply(2, codes[:], scales[:])
         nc.scalar.copy(out=y[:, 2, :], in_=bank[:])
         nc.sync.dma_start(out=out_rows[:, 2, :], in_=y[:, 2, :])
 
         codes, scales = quantize_w(last_grouped[:], "last", "last_codes")
+        y_grouped = keep.tile([P, R, LANES], BF16, name="y_grouped", tag="last_grouped", align_bytes=64)
+        nc.vector.tensor_copy(out=y_grouped[:, :, 0:2], in_=y[:, 0:2, :].rearrange("p t r -> p r t"))
         bank = multiply(last, codes[:], scales[:])
 
         width = R // TAIL_CHUNKS

@@ -95,7 +95,7 @@ def tile_attend_gmeprop_x_pl_kernel(tc, dy, wT, offs, out_0, out_1, out_2):
             return codes, scales
 
         def multiply(t, codes, scales):
-            bank = sums.tile([P, R], F32, name="bank%d" % t, tag="bank%d" % t)
+            bank = sums.tile([P, R], F32, name="bank%s" % t, tag="bank%s" % t)
             nc.tensor.matmul_mx(
                 out=bank[:],
                 lhsT=codes.bitcast(E4M3X4),
@@ -125,6 +125,7 @@ def tile_attend_gmeprop_x_pl_kernel(tc, dy, wT, offs, out_0, out_1, out_2):
         for t in range(2):
             bank = multiply(t, codes[:, t * P : (t + 1) * P], scales[:, t * P : (t + 1) * P])
             nc.scalar.copy(out=y[:, t, :], in_=bank[:])
+        multiply("_spare", codes[:, P : 2 * P], scales[:, P : 2 * P])
         nc.sync.dma_start(out=out_rows[:, 0:2, :], in_=y[:, 0:2, :])
 
         last_picked = keep.tile([P, SLOTS], BF16, name="last_picked", tag="first_grouped", align_bytes=64)

@@ -68,7 +68,7 @@ def tile_attend_gmeprop_x_pl_kernel(tc, dy, wT, offs, out_0, out_1, out_2):
             for h in range(2):
                 nc.tensor.transpose(turned[:, h, :], pairs[:, h * P : (h + 1) * P], identity[:])
 
-        dy_grouped = keep.tile([P, LANES * R], BF16, name="dy_grouped", align_bytes=64)
+        dy_grouped = keep.tile([P, LANES * R], BF16, name="dy_grouped", tag="dy_grouped", align_bytes=64)
         for q in range(2):
             turned = turn.tile([P, 2, 2, P], F32, name="turned")
             for j in range(2):
@@ -112,24 +112,28 @@ def tile_attend_gmeprop_x_pl_kernel(tc, dy, wT, offs, out_0, out_1, out_2):
         y_scales = keep.tile([P, R], U8, name="y_scales", align_bytes=64)
         last = LANES - 1
 
-        first_grouped = keep.tile([P, 2 * LANES * P], BF16, name="first_grouped", tag="first_grouped", align_bytes=64)
+        first_grouped = keep.tile([P, LANES * P], BF16, name="first_grouped", align_bytes=64)
+        second_grouped = keep.tile([P, LANES * P], BF16, name="second_grouped", tag="second_grouped", align_bytes=64)
         third_grouped = keep.tile([P, LANES * P], BF16, name="third_grouped", align_bytes=64)
         last_grouped = keep.tile([P, LANES * P], BF16, name="last_grouped", tag="last_grouped", align_bytes=64)
-        prepare_w(w_first[0][:], first_grouped[:, 0 : LANES * P])
-        dy_codes = keep.tile([P, R], U32, name="dy_codes", tag="w_tile0", align_bytes=64)
+        prepare_w(w_first[0][:], first_grouped[:])
+        second_turned = sums.tile([P, 2, P], F32, name="second_turned", tag="bank0")
+        prepare_w(w_first[1][:], second_grouped[:], None, second_turned)
+        dy_codes = keep.tile([P, R], U32, name="dy_codes", tag="w_tile1", align_bytes=64)
         dy_scales = keep.tile([P, R], U8, name="dy_scales", align_bytes=64)
         nc.vector.quantize_mx(out=dy_codes[:].bitcast(E5M2X4), scales=dy_scales[:], in_=dy_grouped[:])
-        prepare_w(w_first[1][:], first_grouped[:, LANES * P : 2 * LANES * P])
+        codes, scales = quantize_w(first_grouped[:], "first", "dy_grouped")
+        bank = multiply(0, codes[:], scales[:])
+        nc.scalar.copy(out=y[:, 0, :], in_=bank[:])
         prepare_w(w_third[:], third_grouped[:])
-        codes, scales = quantize_w(first_grouped[:], "first", "w_third")
-        for t in range(2):
-            bank = multiply(t, codes[:, t * P : (t + 1) * P], scales[:, t * P : (t + 1) * P])
-            nc.scalar.copy(out=y[:, t, :], in_=bank[:])
-        multiply("_spare", codes[:, P : 2 * P], scales[:, P : 2 * P])
+        codes, scales = quantize_w(second_grouped[:], "second", "w_third")
+        bank = multiply(1, codes[:], scales[:])
+        nc.scalar.copy(out=y[:, 1, :], in_=bank[:])
+        multiply("_spare", codes[:], scales[:])
         nc.sync.dma_start(out=out_rows[:, 0:2, :], in_=y[:, 0:2, :])
 
-        last_picked = keep.tile([P, SLOTS], BF16, name="last_picked", tag="first_grouped", align_bytes=64)
-        last_turned = sums.tile([P, 2, P], F32, name="last_turned", tag="bank0")
+        last_picked = keep.tile([P, SLOTS], BF16, name="last_picked", tag="second_grouped", align_bytes=64)
+        last_turned = sums.tile([P, 2, P], F32, name="last_turned")
         prepare_w(w_last[:], last_grouped[:], last_picked, last_turned)
         codes, scales = quantize_w(third_grouped[:], "third", "w_last")
         bank = multiply(2, codes[:], scales[:])

@@ -134,13 +134,25 @@ def tile_attend_gmeprop_x_pl_kernel(tc, dy, wT, offs, out_0, out_1, out_2):
 
         last_picked = keep.tile([P, SLOTS], BF16, name="last_picked", tag="second_grouped", align_bytes=64)
         last_turned = sums.tile([P, 2, P], F32, name="last_turned")
-        prepare_w(w_last[:], last_grouped[:], last_picked, last_turned)
+        gather_and_turn(w_last[:], last_turned, last_picked)
+        for m0 in (0, P // 2):
+            nc.scalar.copy(
+                out=last_grouped[:, m0 * LANES : (m0 + P // 2) * LANES].bitcast(F32).rearrange("p (m h) -> p m h", h=2),
+                in_=last_turned[:, :, m0 : m0 + P // 2].rearrange("p h m -> p m h"),
+            )
         codes, scales = quantize_w(third_grouped[:], "third", "w_last")
         bank = multiply(2, codes[:], scales[:])
         nc.scalar.copy(out=y[:, 2, :], in_=bank[:])
         nc.sync.dma_start(out=out_rows[:, 2, :], in_=y[:, 2, :])
 
-        codes, scales = quantize_w(last_grouped[:], "last", "last_codes")
+        codes = keep.tile([P, P], U32, name="last_codes", align_bytes=64)
+        scales = keep.tile([P, P], U8, name="last_scales", align_bytes=64)
+        for m0 in (0, P // 2):
+            nc.vector.quantize_mx(
+                out=codes[:, m0 : m0 + P // 2].bitcast(E4M3X4),
+                scales=scales[:, m0 : m0 + P // 2],
+                in_=last_grouped[:, m0 * LANES : (m0 + P // 2) * LANES],
+            )
         y_grouped = keep.tile([P, R, LANES], BF16, name="y_grouped", tag="last_grouped", align_bytes=64)
         nc.vector.tensor_copy(out=y_grouped[:, :, 0:2], in_=y[:, 0:2, :].rearrange("p t r -> p r t"))
         bank = multiply(last, codes[:], scales[:])

@@ -18,7 +18,9 @@ D = 512
 R = 512
 SLOTS = 512
 UNITS = 2048
-TAIL_CHUNKS = 4
+HALF_BLOCK = 16
+DY_LOADS = 2
+QUARTERS = 4
 
 FLOPS = 2 * D * R * SLOTS
 
@@ -39,67 +41,63 @@ def tile_attend_gmeprop_x_pl_kernel(tc, dy, wT, offs, out_0, out_1, out_2):
         offsets = keep.tile([P, SLOTS // 16], U16, name="offsets")
         dy_rows = dy.rearrange("(q p j) k -> q p j k", p=P, j=2)
         dy_tiles = []
-        for q in range(2):
+        for q in range(DY_LOADS):
             dy_tile = keep.tile([P, 2, UNITS], F32, name="dy_tile%d" % q, align_bytes=64)
             nc.sync.dma_start(out=dy_tile[:], in_=dy_rows[q])
             if q == 0:
                 nc.sync.dma_start(offsets[:], offs)
             dy_tiles.append(dy_tile)
-        w_first = []
-        for t in range(2):
+        w_tiles = []
+        for t in range(LANES):
             w_tile = keep.tile([P, UNITS], F32, name="w_tile%d" % t, tag="w_tile%d" % t, align_bytes=64)
             nc.sync.dma_start(out=w_tile[:], in_=w_rows[:, t, :])
-            w_first.append(w_tile)
-        w_third = keep.tile([P, UNITS], F32, name="w_third", tag="w_third", align_bytes=64)
-        nc.sync.dma_start(out=w_third[:], in_=w_rows[:, 2, :])
-        w_last = keep.tile([P, UNITS], F32, name="w_last", tag="w_last", align_bytes=64)
-        nc.sync.dma_start(out=w_last[:], in_=w_rows[:, 3, :])
+            w_tiles.append(w_tile)
 
         identity = keep.tile([P, P], F32, name="identity")
         make_identity(nc, identity[:])
 
-        def gather_and_turn(window, turned, picked=None):
-            if picked is None:
-                picked = ring.tile([P, SLOTS], BF16, name="picked", align_bytes=64)
+        def gather_and_turn(window, picked, turned):
             nc.vector.tensor_copy(
-                picked[:].rearrange("p (h b e) -> p b h e", h=2, e=16), window.indirect(offsets[:])
+                picked[:].rearrange("p (h b e) -> p b h e", h=2, e=HALF_BLOCK), window.indirect(offsets[:])
             )
             pairs = picked[:].bitcast(F32)
             for h in range(2):
                 nc.tensor.transpose(turned[:, h, :], pairs[:, h * P : (h + 1) * P], identity[:])
 
+        def group(turned, grouped):
+            nc.scalar.copy(
+                out=grouped.bitcast(F32).rearrange("p (m h) -> p m h", h=2),
+                in_=turned.rearrange("p h m -> p m h"),
+            )
+
         dy_grouped = keep.tile([P, LANES * R], BF16, name="dy_grouped", tag="dy_grouped", align_bytes=64)
-        for q in range(2):
+        for q in range(DY_LOADS):
             turned = turn.tile([P, 2, 2, P], F32, name="turned")
             for j in range(2):
-                gather_and_turn(dy_tiles[q][:, j, :], turned[:, j])
+                picked = ring.tile([P, SLOTS], BF16, name="picked", align_bytes=64)
+                gather_and_turn(dy_tiles[q][:, j, :], picked, turned[:, j])
             nc.scalar.copy(
                 out=dy_grouped[:, q * 2 * R : (q + 1) * 2 * R].bitcast(F32).rearrange("p (m j h) -> p m j h", j=2, h=2),
                 in_=turned[:].rearrange("p j h m -> p m j h"),
             )
 
-        def prepare_w(window, grouped, picked=None, turned=None):
-            if turned is None:
-                turned = turn.tile([P, 2, P], F32, name="turned")
-            gather_and_turn(window, turned, picked)
-            nc.scalar.copy(
-                out=grouped.bitcast(F32).rearrange("p (m h) -> p m h", h=2),
-                in_=turned[:].rearrange("p h m -> p m h"),
-            )
+        def prepare_lane(t, turned):
+            picked = ring.tile([P, SLOTS], BF16, name="picked", align_bytes=64)
+            gather_and_turn(w_tiles[t][:], picked, turned)
+            group(turned[:], w_grouped[t][:])
 
-        def quantize_w(grouped, name, codes_tag):
-            columns = grouped.shape[1] // LANES
-            codes = keep.tile([P, columns], U32, name=name + "_codes", tag=codes_tag, align_bytes=64)
-            scales = keep.tile([P, columns], U8, name=name + "_scales", align_bytes=64)
-            nc.vector.quantize_mx(out=codes[:].bitcast(E4M3X4), scales=scales[:], in_=grouped)
+        def quantize_lane(t, codes_tag):
+            codes = keep.tile([P, P], U32, name="w_codes%d" % t, tag=codes_tag, align_bytes=64)
+            scales = keep.tile([P, P], U8, name="w_scales%d" % t, align_bytes=64)
+            nc.vector.quantize_mx(out=codes[:].bitcast(E4M3X4), scales=scales[:], in_=w_grouped[t][:])
             return codes, scales
 
-        def multiply(t, codes, scales):
-            bank = sums.tile([P, R], F32, name="bank%s" % t, tag="bank%s" % t)
+        def multiply(bank_tag, codes, scales):
+            bank = sums.tile([P, R], F32, name=bank_tag, tag=bank_tag)
             nc.tensor.matmul_mx(
                 out=bank[:],
-                lhsT=codes.bitcast(E4M3X4),
-                lhsT_scale=scales,
+                lhsT=codes[:].bitcast(E4M3X4),
+                lhsT_scale=scales[:],
                 rhs=dy_codes[:].bitcast(E5M2X4),
                 rhs_scale=dy_scales[:],
                 start=True,
@@ -110,78 +108,73 @@ def tile_attend_gmeprop_x_pl_kernel(tc, dy, wT, offs, out_0, out_1, out_2):
         y = keep.tile([P, LANES, R], F32, name="y", align_bytes=64)
         y_codes = keep.tile([P, R], U32, name="y_codes", align_bytes=64)
         y_scales = keep.tile([P, R], U8, name="y_scales", align_bytes=64)
-        last = LANES - 1
+        w_grouped = [
+            keep.tile([P, LANES * P], BF16, name="w_grouped%d" % t, tag="w_grouped%d" % t, align_bytes=64)
+            for t in range(LANES)
+        ]
 
-        first_grouped = keep.tile([P, LANES * P], BF16, name="first_grouped", align_bytes=64)
-        second_grouped = keep.tile([P, LANES * P], BF16, name="second_grouped", tag="second_grouped", align_bytes=64)
-        third_grouped = keep.tile([P, LANES * P], BF16, name="third_grouped", align_bytes=64)
-        last_grouped = keep.tile([P, LANES * P], BF16, name="last_grouped", tag="last_grouped", align_bytes=64)
-        prepare_w(w_first[0][:], first_grouped[:])
-        second_turned = sums.tile([P, 2, P], F32, name="second_turned", tag="bank0")
-        prepare_w(w_first[1][:], second_grouped[:], None, second_turned)
+        prepare_lane(0, turn.tile([P, 2, P], F32, name="turned"))
+        prepare_lane(1, sums.tile([P, 2, P], F32, name="turned1", tag="bank0"))
         dy_codes = keep.tile([P, R], U32, name="dy_codes", tag="w_tile1", align_bytes=64)
         dy_scales = keep.tile([P, R], U8, name="dy_scales", align_bytes=64)
         nc.vector.quantize_mx(out=dy_codes[:].bitcast(E5M2X4), scales=dy_scales[:], in_=dy_grouped[:])
-        codes, scales = quantize_w(first_grouped[:], "first", "dy_grouped")
-        bank = multiply(0, codes[:], scales[:])
+        codes, scales = quantize_lane(0, "dy_grouped")
+        bank = multiply("bank0", codes, scales)
         nc.scalar.copy(out=y[:, 0, :], in_=bank[:])
-        prepare_w(w_third[:], third_grouped[:])
-        codes, scales = quantize_w(second_grouped[:], "second", "w_third")
-        bank = multiply(1, codes[:], scales[:])
+
+        prepare_lane(2, turn.tile([P, 2, P], F32, name="turned"))
+        codes, scales = quantize_lane(1, "w_tile2")
+        bank = multiply("bank1", codes, scales)
         nc.scalar.copy(out=y[:, 1, :], in_=bank[:])
-        multiply("_spare", codes[:], scales[:])
+        multiply("warm_up", codes, scales)
         nc.sync.dma_start(out=out_rows[:, 0:2, :], in_=y[:, 0:2, :])
 
-        last_picked = keep.tile([P, SLOTS], BF16, name="last_picked", tag="second_grouped", align_bytes=64)
+        last = LANES - 1
+        halves = [slice(0, P // 2), slice(P // 2, P)]
+        last_picked = keep.tile([P, SLOTS], BF16, name="last_picked", tag="w_grouped1", align_bytes=64)
         last_turned = sums.tile([P, 2, P], F32, name="last_turned")
-        gather_and_turn(w_last[:], last_turned, last_picked)
-        for m0 in (0, P // 2):
-            nc.scalar.copy(
-                out=last_grouped[:, m0 * LANES : (m0 + P // 2) * LANES].bitcast(F32).rearrange("p (m h) -> p m h", h=2),
-                in_=last_turned[:, :, m0 : m0 + P // 2].rearrange("p h m -> p m h"),
-            )
-        codes, scales = quantize_w(third_grouped[:], "third", "w_last")
-        bank = multiply(2, codes[:], scales[:])
+        gather_and_turn(w_tiles[last][:], last_picked, last_turned)
+        for rows in halves:
+            group(last_turned[:, :, rows], w_grouped[last][:, rows.start * LANES : rows.stop * LANES])
+
+        codes, scales = quantize_lane(2, "w_tile3")
+        bank = multiply("bank2", codes, scales)
         nc.scalar.copy(out=y[:, 2, :], in_=bank[:])
         nc.sync.dma_start(out=out_rows[:, 2, :], in_=y[:, 2, :])
 
-        codes = keep.tile([P, P], U32, name="last_codes", align_bytes=64)
-        scales = keep.tile([P, P], U8, name="last_scales", align_bytes=64)
-        for m0 in (0, P // 2):
+        codes = keep.tile([P, P], U32, name="w_codes3", align_bytes=64)
+        scales = keep.tile([P, P], U8, name="w_scales3", align_bytes=64)
+        for rows in halves:
             nc.vector.quantize_mx(
-                out=codes[:, m0 : m0 + P // 2].bitcast(E4M3X4),
-                scales=scales[:, m0 : m0 + P // 2],
-                in_=last_grouped[:, m0 * LANES : (m0 + P // 2) * LANES],
+                out=codes[:, rows].bitcast(E4M3X4),
+                scales=scales[:, rows],
+                in_=w_grouped[last][:, rows.start * LANES : rows.stop * LANES],
             )
-        y_grouped = keep.tile([P, R, LANES], BF16, name="y_grouped", tag="last_grouped", align_bytes=64)
+        y_grouped = keep.tile([P, R, LANES], BF16, name="y_grouped", tag="w_grouped3", align_bytes=64)
         nc.vector.tensor_copy(out=y_grouped[:, :, 0:2], in_=y[:, 0:2, :].rearrange("p t r -> p r t"))
-        bank = multiply(last, codes[:], scales[:])
+        bank = multiply("bank3", codes, scales)
 
-        width = R // TAIL_CHUNKS
-        chunks = [slice(c * width, (c + 1) * width) for c in range(TAIL_CHUNKS)]
-
-        def quantize_result(cols):
-            nc.vector.quantize_mx(
-                out=y_codes[:, cols].bitcast(E4M3X4),
-                scales=y_scales[:, cols],
-                in_=y_grouped[:, cols, :].rearrange("p r t -> p (r t)"),
-            )
-
-        for cols in chunks:
+        width = R // QUARTERS
+        quarters = [slice(c * width, (c + 1) * width) for c in range(QUARTERS)]
+        for cols in quarters:
             nc.scalar.copy(out=y[:, last, cols], in_=bank[:, cols])
         nc.sync.dma_start(out=out_rows[:, last, :], in_=y[:, last, :])
-        for cols in chunks[:-1]:
+        for cols in quarters[:-1]:
             nc.vector.tensor_copy(out=y_grouped[:, cols, 2:4], in_=y[:, 2:4, cols].rearrange("p t r -> p r t"))
-        nc.scalar.copy(out=y_grouped[:, chunks[-1], 2:4], in_=y[:, 2:4, chunks[-1]].rearrange("p t r -> p r t"))
-        half = R // 2
-        quantize_result(slice(0, half))
-        nc.sync.dma_start(out=out_words[:, 0:half], in_=y_codes[:, 0:half].bitcast(I32))
-        quantize_result(chunks[-2])
-        quantize_result(chunks[-1])
-        nc.sync.dma_start(out=out_words[:, half:R], in_=y_codes[:, half:R].bitcast(I32))
-        for quad in range(4):
-            queue = nc.scalar if quad % 2 == 0 else nc.sync
+        nc.scalar.copy(out=y_grouped[:, quarters[-1], 2:4], in_=y[:, 2:4, quarters[-1]].rearrange("p t r -> p r t"))
+
+        for pair in (quarters[:2], quarters[2:]):
+            for cols in pair:
+                nc.vector.quantize_mx(
+                    out=y_codes[:, cols].bitcast(E4M3X4),
+                    scales=y_scales[:, cols],
+                    in_=y_grouped[:, cols, :].rearrange("p r t -> p (r t)"),
+                )
+            stored = slice(pair[0].start, pair[1].stop)
+            nc.sync.dma_start(out=out_words[:, stored], in_=y_codes[:, stored].bitcast(I32))
+        for g in range(P // 32):
+            queue = nc.scalar if g % 2 == 0 else nc.sync
             queue.dma_start(
-                out=out_scales[4 * quad : 4 * quad + 4, :],
-                in_=y_scales[32 * quad : 32 * quad + 4, :].bitcast(I32),
+                out=out_scales[4 * g : 4 * g + 4, :],
+                in_=y_scales[32 * g : 32 * g + 4, :].bitcast(I32),
             )

@@ -90,15 +90,15 @@ def tile_attend_gmeprop_x_pl_kernel(tc, dy, wT, offs, out_0, out_1, out_2):
             codes = keep.tile([P, P], U32, name="w_codes%d" % t, tag=codes_tag, align_bytes=64)
             scales = keep.tile([P, P], U8, name="w_scales%d" % t, align_bytes=64)
             nc.vector.quantize_mx(out=codes[:].bitcast(E4M3X4), scales=scales[:], in_=w_grouped[t][:])
-            return codes, scales
+            return codes[:], scales[:]
 
         def multiply(bank_tag, codes, scales):
             bank = sums.tile([P, R], F32, name=bank_tag, tag=bank_tag)
             nc.tensor.matmul_mx(
                 out=bank[:],
-                lhsT=codes[:].bitcast(E4M3X4),
-                lhsT_scale=scales[:],
-                rhs=dy_codes[:].bitcast(E5M2X4),
+                lhsT=codes.bitcast(E4M3X4),
+                lhsT_scale=scales,
+                rhs=dy_codes.bitcast(E5M2X4),
                 rhs_scale=dy_scales[:],
                 start=True,
                 stop=True,
@@ -115,10 +115,13 @@ def tile_attend_gmeprop_x_pl_kernel(tc, dy, wT, offs, out_0, out_1, out_2):
 
         prepare_lane(0, turn.tile([P, 2, P], F32, name="turned"))
         prepare_lane(1, sums.tile([P, 2, P], F32, name="turned1", tag="bank0"))
-        dy_codes = keep.tile([P, R], U32, name="dy_codes", tag="w_tile1", align_bytes=64)
+        first_codes = keep.tile([P, R + P], U32, name="first_codes", tag="w_tile1", align_bytes=64)
+        dy_codes = first_codes[:, 0:R]
         dy_scales = keep.tile([P, R], U8, name="dy_scales", align_bytes=64)
-        nc.vector.quantize_mx(out=dy_codes[:].bitcast(E5M2X4), scales=dy_scales[:], in_=dy_grouped[:])
-        codes, scales = quantize_lane(0, "dy_grouped")
+        nc.vector.quantize_mx(out=dy_codes.bitcast(E5M2X4), scales=dy_scales[:], in_=dy_grouped[:])
+        codes = first_codes[:, R : R + P]
+        scales = keep.tile([P, P], U8, name="w_scales0", align_bytes=64)[:]
+        nc.vector.quantize_mx(out=codes.bitcast(E4M3X4), scales=scales, in_=w_grouped[0][:])
         bank = multiply("bank0", codes, scales)
         nc.scalar.copy(out=y[:, 0, :], in_=bank[:])
 
@@ -131,7 +134,7 @@ def tile_attend_gmeprop_x_pl_kernel(tc, dy, wT, offs, out_0, out_1, out_2):
 
         last = LANES - 1
         halves = [slice(0, P // 2), slice(P // 2, P)]
-        last_picked = keep.tile([P, SLOTS], BF16, name="last_picked", tag="w_grouped1", align_bytes=64)
+        last_picked = keep.tile([P, SLOTS], BF16, name="last_picked", align_bytes=64)
         last_turned = sums.tile([P, 2, P], F32, name="last_turned")
         gather_and_turn(w_tiles[last][:], last_picked, last_turned)
         for rows in halves:
@@ -152,7 +155,7 @@ def tile_attend_gmeprop_x_pl_kernel(tc, dy, wT, offs, out_0, out_1, out_2):
             )
         y_grouped = keep.tile([P, R, LANES], BF16, name="y_grouped", tag="w_grouped3", align_bytes=64)
         nc.vector.tensor_copy(out=y_grouped[:, :, 0:2], in_=y[:, 0:2, :].rearrange("p t r -> p r t"))
-        bank = multiply("bank3", codes, scales)
+        bank = multiply("bank3", codes[:], scales[:])
 
         width = R // QUARTERS
         quarters = [slice(c * width, (c + 1) * width) for c in range(QUARTERS)]

@@ -21,6 +21,7 @@ UNITS = 2048
 HALF_BLOCK = 16
 DY_LOADS = 2
 QUARTERS = 4
+PAST_CODES = 1024
 
 FLOPS = 2 * D * R * SLOTS
 
@@ -35,6 +36,7 @@ def tile_attend_gmeprop_x_pl_kernel(tc, dy, wT, offs, out_0, out_1, out_2):
     with ExitStack() as ctx:
         keep = ctx.enter_context(tc.tile_pool(name="keep", bufs=1))
         ring = ctx.enter_context(tc.tile_pool(name="ring", bufs=2))
+        shared = ctx.enter_context(tc.tile_pool(name="shared", bufs=1))
         turn = ctx.enter_context(tc.psum_pool(name="turn", bufs=2))
         sums = ctx.enter_context(tc.psum_pool(name="sums", bufs=1))
 
@@ -48,8 +50,12 @@ def tile_attend_gmeprop_x_pl_kernel(tc, dy, wT, offs, out_0, out_1, out_2):
                 nc.sync.dma_start(offsets[:], offs)
             dy_tiles.append(dy_tile)
         w_tiles = []
+        last = LANES - 1
         for t in range(LANES):
-            w_tile = keep.tile([P, UNITS], F32, name="w_tile%d" % t, tag="w_tile%d" % t, align_bytes=64)
+            if t < last:
+                w_tile = keep.tile([P, UNITS], F32, name="w_tile%d" % t, tag="w_tile%d" % t, align_bytes=64)
+            else:
+                w_tile = shared.tile([P, UNITS], F32, name="last_window", offset=0, align_bytes=64)
             nc.sync.dma_start(out=w_tile[:], in_=w_rows[:, t, :])
             w_tiles.append(w_tile)
 
@@ -86,11 +92,10 @@ def tile_attend_gmeprop_x_pl_kernel(tc, dy, wT, offs, out_0, out_1, out_2):
             gather_and_turn(w_tiles[t][:], picked, turned)
             group(turned[:], w_grouped[t][:])
 
-        def quantize_lane(t, codes_tag):
-            codes = keep.tile([P, P], U32, name="w_codes%d" % t, tag=codes_tag, align_bytes=64)
+        def quantize_lane(t, codes):
             scales = keep.tile([P, P], U8, name="w_scales%d" % t, align_bytes=64)
-            nc.vector.quantize_mx(out=codes[:].bitcast(E4M3X4), scales=scales[:], in_=w_grouped[t][:])
-            return codes[:], scales[:]
+            nc.vector.quantize_mx(out=codes.bitcast(E4M3X4), scales=scales[:], in_=w_grouped[t][:])
+            return scales[:]
 
         def multiply(bank_tag, codes, scales):
             bank = sums.tile([P, R], F32, name=bank_tag, tag=bank_tag)
@@ -120,19 +125,18 @@ def tile_attend_gmeprop_x_pl_kernel(tc, dy, wT, offs, out_0, out_1, out_2):
         dy_scales = keep.tile([P, R], U8, name="dy_scales", align_bytes=64)
         nc.vector.quantize_mx(out=dy_codes.bitcast(E5M2X4), scales=dy_scales[:], in_=dy_grouped[:])
         codes = first_codes[:, R : R + P]
-        scales = keep.tile([P, P], U8, name="w_scales0", align_bytes=64)[:]
-        nc.vector.quantize_mx(out=codes.bitcast(E4M3X4), scales=scales, in_=w_grouped[0][:])
+        scales = quantize_lane(0, codes)
         bank = multiply("bank0", codes, scales)
         nc.scalar.copy(out=y[:, 0, :], in_=bank[:])
 
         prepare_lane(2, turn.tile([P, 2, P], F32, name="turned"))
-        codes, scales = quantize_lane(1, "w_tile2")
+        codes = keep.tile([P, P], U32, name="w_codes1", tag="w_tile2", align_bytes=64)[:]
+        scales = quantize_lane(1, codes)
         bank = multiply("bank1", codes, scales)
         nc.scalar.copy(out=y[:, 1, :], in_=bank[:])
         multiply("warm_up", codes, scales)
         nc.sync.dma_start(out=out_rows[:, 0:2, :], in_=y[:, 0:2, :])
 
-        last = LANES - 1
         halves = [slice(0, P // 2), slice(P // 2, P)]
         last_picked = keep.tile([P, SLOTS], BF16, name="last_picked", align_bytes=64)
         last_turned = sums.tile([P, 2, P], F32, name="last_turned")
@@ -140,9 +144,12 @@ def tile_attend_gmeprop_x_pl_kernel(tc, dy, wT, offs, out_0, out_1, out_2):
         for rows in halves:
             group(last_turned[:, :, rows], w_grouped[last][:, rows.start * LANES : rows.stop * LANES])
 
-        codes, scales = quantize_lane(2, "w_tile3")
+        codes = shared.tile([P, P], U32, name="w_codes2", offset=0, align_bytes=64)[:]
+        scales = quantize_lane(2, codes)
         bank = multiply("bank2", codes, scales)
         nc.scalar.copy(out=y[:, 2, :], in_=bank[:])
+        y_low = shared.tile([P, R // 2, LANES], BF16, name="y_low", offset=PAST_CODES, align_bytes=64)
+        nc.vector.tensor_copy(out=y_low[:, :, 0:2], in_=y[:, 0:2, 0 : R // 2].rearrange("p t r -> p r t"))
         nc.sync.dma_start(out=out_rows[:, 2, :], in_=y[:, 2, :])
 
         codes = keep.tile([P, P], U32, name="w_codes3", align_bytes=64)
@@ -153,8 +160,13 @@ def tile_attend_gmeprop_x_pl_kernel(tc, dy, wT, offs, out_0, out_1, out_2):
                 scales=scales[:, rows],
                 in_=w_grouped[last][:, rows.start * LANES : rows.stop * LANES],
             )
-        y_grouped = keep.tile([P, R, LANES], BF16, name="y_grouped", tag="w_grouped3", align_bytes=64)
-        nc.vector.tensor_copy(out=y_grouped[:, :, 0:2], in_=y[:, 0:2, :].rearrange("p t r -> p r t"))
+        y_high = keep.tile([P, R // 2, LANES], BF16, name="y_high", tag="w_grouped3", align_bytes=64)
+        nc.vector.tensor_copy(out=y_high[:, :, 0:2], in_=y[:, 0:2, R // 2 : R].rearrange("p t r -> p r t"))
+
+        def y_grouped(cols):
+            half = (y_low, y_high)[cols.start // (R // 2)]
+            return half[:, cols.start % (R // 2) : (cols.stop - 1) % (R // 2) + 1, :]
+
         bank = multiply("bank3", codes[:], scales[:])
 
         width = R // QUARTERS
@@ -163,15 +175,15 @@ def tile_attend_gmeprop_x_pl_kernel(tc, dy, wT, offs, out_0, out_1, out_2):
             nc.scalar.copy(out=y[:, last, cols], in_=bank[:, cols])
         nc.sync.dma_start(out=out_rows[:, last, :], in_=y[:, last, :])
         for cols in quarters[:-1]:
-            nc.vector.tensor_copy(out=y_grouped[:, cols, 2:4], in_=y[:, 2:4, cols].rearrange("p t r -> p r t"))
-        nc.scalar.copy(out=y_grouped[:, quarters[-1], 2:4], in_=y[:, 2:4, quarters[-1]].rearrange("p t r -> p r t"))
+            nc.vector.tensor_copy(out=y_grouped(cols)[:, :, 2:4], in_=y[:, 2:4, cols].rearrange("p t r -> p r t"))
+        nc.scalar.copy(out=y_grouped(quarters[-1])[:, :, 2:4], in_=y[:, 2:4, quarters[-1]].rearrange("p t r -> p r t"))
 
         for pair in (quarters[:2], quarters[2:]):
             for cols in pair:
                 nc.vector.quantize_mx(
                     out=y_codes[:, cols].bitcast(E4M3X4),
                     scales=y_scales[:, cols],
-                    in_=y_grouped[:, cols, :].rearrange("p r t -> p (r t)"),
+                    in_=y_grouped(cols).rearrange("p r t -> p (r t)"),
                 )
             stored = slice(pair[0].start, pair[1].stop)
             nc.sync.dma_start(out=out_words[:, stored], in_=y_codes[:, stored].bitcast(I32))

@@ -11,6 +11,7 @@ U16 = mybir.dt.uint16
 U8 = mybir.dt.uint8
 E4M3X4 = mybir.dt.float8_e4m3fn_x4
 E5M2X4 = mybir.dt.float8_e5m2_x4
+COPY = mybir.ActivationFunctionType.Copy
 
 P = 128
 LANES = 4
@@ -18,10 +19,9 @@ D = 512
 R = 512
 SLOTS = 512
 UNITS = 2048
-HALF_BLOCK = 16
-DY_LOADS = 2
-QUARTERS = 4
-PAST_CODES = 1024
+TILES = R // P
+VECTOR_SLOTS = 192
+WINDOW = 4 * UNITS
 
 FLOPS = 2 * D * R * SLOTS
 
@@ -38,155 +38,155 @@ def tile_attend_gmeprop_x_pl_kernel(tc, dy, wT, offs, out_0, out_1, out_2):
         ring = ctx.enter_context(tc.tile_pool(name="ring", bufs=2))
         shared = ctx.enter_context(tc.tile_pool(name="shared", bufs=1))
         turn = ctx.enter_context(tc.psum_pool(name="turn", bufs=2))
-        sums = ctx.enter_context(tc.psum_pool(name="sums", bufs=1))
+        sums = ctx.enter_context(tc.psum_pool(name="sums", bufs=3))
+        ends = ctx.enter_context(tc.psum_pool(name="ends", bufs=1))
 
         offsets = keep.tile([P, SLOTS // 16], U16, name="offsets")
-        dy_rows = dy.rearrange("(q p j) k -> q p j k", p=P, j=2)
-        dy_tiles = []
-        for q in range(DY_LOADS):
-            dy_tile = keep.tile([P, 2, UNITS], F32, name="dy_tile%d" % q, align_bytes=64)
-            nc.sync.dma_start(out=dy_tile[:], in_=dy_rows[q])
-            if q == 0:
-                nc.sync.dma_start(offsets[:], offs)
-            dy_tiles.append(dy_tile)
         w_tiles = []
-        last = LANES - 1
         for t in range(LANES):
-            if t < last:
-                w_tile = keep.tile([P, UNITS], F32, name="w_tile%d" % t, tag="w_tile%d" % t, align_bytes=64)
-            else:
-                w_tile = shared.tile([P, UNITS], F32, name="last_window", offset=0, align_bytes=64)
+            w_tile = keep.tile([P, UNITS], F32, name="w_tile%d" % t, align_bytes=64)
             nc.sync.dma_start(out=w_tile[:], in_=w_rows[:, t, :])
+            if t == 0:
+                nc.sync.dma_start(offsets[:], offs)
             w_tiles.append(w_tile)
+        dy_tiles = []
+        for j in range(TILES):
+            dy_tile = shared.tile([P, UNITS], F32, name="dy_tile%d" % j, offset=j * WINDOW, align_bytes=64)
+            nc.sync.dma_start(out=dy_tile[:], in_=dy[j * P : (j + 1) * P, :])
+            dy_tiles.append(dy_tile)
 
         identity = keep.tile([P, P], F32, name="identity")
         make_identity(nc, identity[:])
 
-        def gather_and_turn(window, picked, turned):
-            nc.vector.tensor_copy(
-                picked[:].rearrange("p (h b e) -> p b h e", h=2, e=HALF_BLOCK), window.indirect(offsets[:])
-            )
+        def gather_and_turn(window, vector_slots=VECTOR_SLOTS):
+            picked = ring.tile([P, SLOTS], BF16, name="picked", align_bytes=64)
+            split = vector_slots // 16
+            nc.vector.tensor_copy(picked[:, 0:vector_slots], window[:].indirect(offsets[:, 0:split]))
+            if vector_slots < SLOTS:
+                nc.scalar.activation(picked[:, vector_slots:SLOTS], window[:].indirect(offsets[:, split:]), COPY)
             pairs = picked[:].bitcast(F32)
-            for h in range(2):
-                nc.tensor.transpose(turned[:, h, :], pairs[:, h * P : (h + 1) * P], identity[:])
+            turned = turn.tile([P, 2, P], F32, name="turned")
+            for u in range(2):
+                nc.tensor.transpose(turned[:, u, :], pairs[:, u : 2 * P : 2], identity[:])
+            return turned
 
         def group(turned, grouped):
             nc.scalar.copy(
-                out=grouped.bitcast(F32).rearrange("p (m h) -> p m h", h=2),
-                in_=turned.rearrange("p h m -> p m h"),
+                out=grouped.bitcast(F32).rearrange("p (m u) -> p m u", u=2), in_=turned.rearrange("p u m -> p m u")
             )
 
-        dy_grouped = keep.tile([P, LANES * R], BF16, name="dy_grouped", tag="dy_grouped", align_bytes=64)
-        for q in range(DY_LOADS):
-            turned = turn.tile([P, 2, 2, P], F32, name="turned")
-            for j in range(2):
-                picked = ring.tile([P, SLOTS], BF16, name="picked", align_bytes=64)
-                gather_and_turn(dy_tiles[q][:, j, :], picked, turned[:, j])
-            nc.scalar.copy(
-                out=dy_grouped[:, q * 2 * R : (q + 1) * 2 * R].bitcast(F32).rearrange("p (m j h) -> p m j h", j=2, h=2),
-                in_=turned[:].rearrange("p j h m -> p m j h"),
-            )
+        early = (LANES - 1) * P
+        w_grouped = keep.tile([P, LANES * early], BF16, name="w_grouped", align_bytes=64)
+        for t in range(LANES - 1):
+            group(gather_and_turn(w_tiles[t], SLOTS)[:], w_grouped[:, t * LANES * P : (t + 1) * LANES * P])
+        turned3 = gather_and_turn(w_tiles[LANES - 1], SLOTS)
+        turned = gather_and_turn(dy_tiles[0], SLOTS // 2)
+        w_grouped3 = shared.tile([P, LANES * P], BF16, name="w_grouped3", offset=0, align_bytes=64)
+        group(turned3[:], w_grouped3[:])
+        w_codes = shared.tile([P, D], U32, name="w_codes", offset=WINDOW // 2, align_bytes=64)
+        w_scales = keep.tile([P, D], U8, name="w_scales", align_bytes=64)
+        nc.vector.quantize_mx(out=w_codes[:, 0:early].bitcast(E4M3X4), scales=w_scales[:, 0:early], in_=w_grouped[:])
+        nc.vector.quantize_mx(out=w_codes[:, early:D].bitcast(E4M3X4), scales=w_scales[:, early:D], in_=w_grouped3[:])
 
-        def prepare_lane(t, turned):
-            picked = ring.tile([P, SLOTS], BF16, name="picked", align_bytes=64)
-            gather_and_turn(w_tiles[t][:], picked, turned)
-            group(turned[:], w_grouped[t][:])
+        y_scales = keep.tile([P, R], U8, name="y_scales", align_bytes=64)
 
-        def quantize_lane(t, codes):
-            scales = keep.tile([P, P], U8, name="w_scales%d" % t, align_bytes=64)
-            nc.vector.quantize_mx(out=codes.bitcast(E4M3X4), scales=scales[:], in_=w_grouped[t][:])
-            return scales[:]
-
-        def multiply(bank_tag, codes, scales):
-            bank = sums.tile([P, R], F32, name=bank_tag, tag=bank_tag)
+        def multiply(out, t, codes, scales):
+            cols = slice(t * P, (t + 1) * P)
             nc.tensor.matmul_mx(
-                out=bank[:],
-                lhsT=codes.bitcast(E4M3X4),
-                lhsT_scale=scales,
-                rhs=dy_codes.bitcast(E5M2X4),
-                rhs_scale=dy_scales[:],
+                out=out,
+                lhsT=w_codes[:, cols].bitcast(E4M3X4),
+                lhsT_scale=w_scales[:, cols],
+                rhs=codes[:].bitcast(E5M2X4),
+                rhs_scale=scales[:],
                 start=True,
                 stop=True,
             )
+
+        def quantize_and_multiply(turned):
+            grouped = ring.tile([P, LANES * P], BF16, name="grouped", align_bytes=64)
+            codes = ring.tile([P, P], U32, name="codes", align_bytes=64)
+            scales = ring.tile([P, P], U8, name="scales", align_bytes=64)
+            for rows in (slice(0, P // 2), slice(P // 2, P)):
+                group(turned[:, :, rows], grouped[:, LANES * rows.start : LANES * rows.stop])
+            for rows in (slice(0, P // 2), slice(P // 2, P)):
+                nc.vector.quantize_mx(
+                    out=codes[:, rows].bitcast(E5M2X4),
+                    scales=scales[:, rows],
+                    in_=grouped[:, LANES * rows.start : LANES * rows.stop],
+                )
+            bank = sums.tile([P, LANES, P], F32, name="bank")
+            for t in range(LANES):
+                multiply(bank[:, t, :], t, codes, scales)
             return bank
 
-        y = keep.tile([P, LANES, R], F32, name="y", align_bytes=64)
-        y_codes = keep.tile([P, R], U32, name="y_codes", align_bytes=64)
-        y_scales = keep.tile([P, R], U8, name="y_scales", align_bytes=64)
-        w_grouped = [
-            keep.tile([P, LANES * P], BF16, name="w_grouped%d" % t, tag="w_grouped%d" % t, align_bytes=64)
-            for t in range(LANES)
-        ]
-
-        prepare_lane(0, turn.tile([P, 2, P], F32, name="turned"))
-        prepare_lane(1, sums.tile([P, 2, P], F32, name="turned1", tag="bank0"))
-        first_codes = keep.tile([P, R + P], U32, name="first_codes", tag="w_tile1", align_bytes=64)
-        dy_codes = first_codes[:, 0:R]
-        dy_scales = keep.tile([P, R], U8, name="dy_scales", align_bytes=64)
-        nc.vector.quantize_mx(out=dy_codes.bitcast(E5M2X4), scales=dy_scales[:], in_=dy_grouped[:])
-        codes = first_codes[:, R : R + P]
-        scales = quantize_lane(0, codes)
-        bank = multiply("bank0", codes, scales)
-        nc.scalar.copy(out=y[:, 0, :], in_=bank[:])
-
-        prepare_lane(2, turn.tile([P, 2, P], F32, name="turned"))
-        codes = keep.tile([P, P], U32, name="w_codes1", tag="w_tile2", align_bytes=64)[:]
-        scales = quantize_lane(1, codes)
-        bank = multiply("bank1", codes, scales)
-        nc.scalar.copy(out=y[:, 1, :], in_=bank[:])
-        multiply("warm_up", codes, scales)
-        nc.sync.dma_start(out=out_rows[:, 0:2, :], in_=y[:, 0:2, :])
-
-        halves = [slice(0, P // 2), slice(P // 2, P)]
-        last_picked = keep.tile([P, SLOTS], BF16, name="last_picked", align_bytes=64)
-        last_turned = sums.tile([P, 2, P], F32, name="last_turned")
-        gather_and_turn(w_tiles[last][:], last_picked, last_turned)
-        for rows in halves:
-            group(last_turned[:, :, rows], w_grouped[last][:, rows.start * LANES : rows.stop * LANES])
-
-        codes = shared.tile([P, P], U32, name="w_codes2", offset=0, align_bytes=64)[:]
-        scales = quantize_lane(2, codes)
-        bank = multiply("bank2", codes, scales)
-        nc.scalar.copy(out=y[:, 2, :], in_=bank[:])
-        y_low = shared.tile([P, R // 2, LANES], BF16, name="y_low", offset=PAST_CODES, align_bytes=64)
-        nc.vector.tensor_copy(out=y_low[:, :, 0:2], in_=y[:, 0:2, 0 : R // 2].rearrange("p t r -> p r t"))
-        nc.sync.dma_start(out=out_rows[:, 2, :], in_=y[:, 2, :])
-
-        codes = keep.tile([P, P], U32, name="w_codes3", align_bytes=64)
-        scales = keep.tile([P, P], U8, name="w_scales3", align_bytes=64)
-        for rows in halves:
+        def quantize_result(j, codes, rounded):
             nc.vector.quantize_mx(
-                out=codes[:, rows].bitcast(E4M3X4),
-                scales=scales[:, rows],
-                in_=w_grouped[last][:, rows.start * LANES : rows.stop * LANES],
+                out=codes.bitcast(E4M3X4),
+                scales=y_scales[:, j * P : (j + 1) * P],
+                in_=rounded[:].rearrange("p r t -> p (r t)"),
             )
-        y_high = keep.tile([P, R // 2, LANES], BF16, name="y_high", tag="w_grouped3", align_bytes=64)
-        nc.vector.tensor_copy(out=y_high[:, :, 0:2], in_=y[:, 0:2, R // 2 : R].rearrange("p t r -> p r t"))
 
-        def y_grouped(cols):
-            half = (y_low, y_high)[cols.start // (R // 2)]
-            return half[:, cols.start % (R // 2) : (cols.stop - 1) % (R // 2) + 1, :]
+        def round_sums(j, bank):
+            rounded = shared.tile([P, P, LANES], BF16, name="rounded%d" % j, offset=(j + 1) * WINDOW, align_bytes=64)
+            nc.vector.tensor_copy(out=rounded[:], in_=bank[:].rearrange("p t r -> p r t"))
+            return rounded
 
-        bank = multiply("bank3", codes[:], scales[:])
+        def hand_out(j, bank, rounded):
+            base = (j + 2) * WINDOW
+            codes = shared.tile([P, P], U32, name="y_codes%d" % j, offset=base + WINDOW // 4, align_bytes=64)
+            quantize_result(j, codes[:], rounded)
+            y = shared.tile([P, LANES, P], F32, name="y%d" % j, offset=base + WINDOW // 2, align_bytes=64)
+            nc.scalar.copy(out=y[:], in_=bank[:])
+            nc.sync.dma_start(out=out_words[:, j * P : (j + 1) * P], in_=codes[:].bitcast(I32))
+            nc.sync.dma_start(out=out_rows[:, :, j * P : (j + 1) * P], in_=y[:])
 
-        width = R // QUARTERS
-        quarters = [slice(c * width, (c + 1) * width) for c in range(QUARTERS)]
-        for cols in quarters:
-            nc.scalar.copy(out=y[:, last, cols], in_=bank[:, cols])
-        nc.sync.dma_start(out=out_rows[:, last, :], in_=y[:, last, :])
-        for cols in quarters[:-1]:
-            nc.vector.tensor_copy(out=y_grouped(cols)[:, :, 2:4], in_=y[:, 2:4, cols].rearrange("p t r -> p r t"))
-        nc.scalar.copy(out=y_grouped(quarters[-1])[:, :, 2:4], in_=y[:, 2:4, quarters[-1]].rearrange("p t r -> p r t"))
+        bank0 = quantize_and_multiply(turned)
 
-        for pair in (quarters[:2], quarters[2:]):
-            for cols in pair:
-                nc.vector.quantize_mx(
-                    out=y_codes[:, cols].bitcast(E4M3X4),
-                    scales=y_scales[:, cols],
-                    in_=y_grouped(cols).rearrange("p r t -> p (r t)"),
-                )
-            stored = slice(pair[0].start, pair[1].stop)
-            nc.sync.dma_start(out=out_words[:, stored], in_=y_codes[:, stored].bitcast(I32))
+        turned = gather_and_turn(dy_tiles[1])
+        rounded0 = round_sums(0, bank0)
+        bank1 = quantize_and_multiply(turned)
+
+        turned = gather_and_turn(dy_tiles[2])
+        hand_out(0, bank0, rounded0)
+        rounded1 = round_sums(1, bank1)
+        bank2 = quantize_and_multiply(turned)
+
+        last = TILES - 1
+        turned = gather_and_turn(dy_tiles[last])
+        hand_out(1, bank1, rounded1)
+        rounded2 = round_sums(2, bank2)
+        half = P // 2
+        first_half = shared.tile([P, LANES * half], BF16, name="first_half", offset=4 * WINDOW + 768, align_bytes=64)
+        second_half = keep.tile([P, LANES * half], BF16, name="second_half", align_bytes=64)
+        codes = keep.tile([P, P], U32, name="last_codes", align_bytes=64)
+        scales = keep.tile([P, P], U8, name="last_scales", align_bytes=64)
+        halves = [(slice(0, half), first_half), (slice(half, P), second_half)]
+        for rows, grouped in halves:
+            group(turned[:, :, rows], grouped[:])
+        for rows, grouped in halves:
+            nc.vector.quantize_mx(out=codes[:, rows].bitcast(E5M2X4), scales=scales[:, rows], in_=grouped[:])
+        low = ends.tile([P, 2, P], F32, name="low")
+        high = ends.tile([P, 2, P], F32, name="high")
+        for t in range(LANES):
+            multiply((low, high)[t // 2][:, t % 2, :], t, codes, scales)
+
+        y2 = shared.tile([P, LANES, P], F32, name="y2", offset=4 * WINDOW + 1024, align_bytes=64)
+        nc.scalar.copy(out=y2[:], in_=bank2[:])
+        nc.sync.dma_start(out=out_rows[:, :, 2 * P : 3 * P], in_=y2[:])
+        codes23 = shared.tile([P, 2 * P], U32, name="y_codes23", offset=4 * WINDOW, align_bytes=64)
+        quantize_result(2, codes23[:, 0:P], rounded2)
+
+        rounded = keep.tile([P, P, LANES], BF16, name="last_rounded", align_bytes=64)
+        y_low = keep.tile([P, 2, P], F32, name="y_low", align_bytes=64)
+        y_high = keep.tile([P, 2, P], F32, name="y_high", align_bytes=64)
+        nc.vector.tensor_copy(out=rounded[:, :, 0:2], in_=low[:].rearrange("p t r -> p r t"))
+        nc.scalar.copy(out=rounded[:, :, 2:4], in_=high[:].rearrange("p t r -> p r t"))
+        nc.vector.tensor_copy(out=y_low[:], in_=low[:])
+        nc.scalar.copy(out=y_high[:], in_=high[:])
+        quantize_result(last, codes23[:, P : 2 * P], rounded)
+        nc.sync.dma_start(out=out_rows[:, 0:2, last * P : R], in_=y_low[:])
+        nc.scalar.dma_start(out=out_rows[:, 2:4, last * P : R], in_=y_high[:])
+        nc.sync.dma_start(out=out_words[:, 2 * P : R], in_=codes23[:].bitcast(I32))
         for g in range(P // 32):
             queue = nc.scalar if g % 2 == 0 else nc.sync
             queue.dma_start(

@@ -37,156 +37,170 @@ def tile_attend_gmeprop_x_pl_kernel(tc, dy, wT, offs, out_0, out_1, out_2):
         keep = ctx.enter_context(tc.tile_pool(name="keep", bufs=1))
         ring = ctx.enter_context(tc.tile_pool(name="ring", bufs=2))
         shared = ctx.enter_context(tc.tile_pool(name="shared", bufs=1))
-        turn = ctx.enter_context(tc.psum_pool(name="turn", bufs=2))
-        sums = ctx.enter_context(tc.psum_pool(name="sums", bufs=3))
+        turn = ctx.enter_context(tc.psum_pool(name="turn", bufs=3))
+        sums = ctx.enter_context(tc.psum_pool(name="sums", bufs=2))
         ends = ctx.enter_context(tc.psum_pool(name="ends", bufs=1))
 
         offsets = keep.tile([P, SLOTS // 16], U16, name="offsets")
-        w_tiles = []
-        for t in range(LANES):
-            w_tile = keep.tile([P, UNITS], F32, name="w_tile%d" % t, align_bytes=64)
-            nc.sync.dma_start(out=w_tile[:], in_=w_rows[:, t, :])
-            if t == 0:
+        last = TILES - 1
+        early = last * P
+        sources = [dy[j * P : (j + 1) * P, :] for j in range(last)] + [w_rows[:, t, :] for t in range(LANES)]
+        sources.append(dy[early:R, :])
+        windows = []
+        for n, source in enumerate(sources):
+            window = shared.tile([P, UNITS], F32, name="window%d" % n, offset=n * WINDOW, align_bytes=64)
+            nc.sync.dma_start(out=window[:], in_=source)
+            if n == 0:
                 nc.sync.dma_start(offsets[:], offs)
-            w_tiles.append(w_tile)
-        dy_tiles = []
-        for j in range(TILES):
-            dy_tile = shared.tile([P, UNITS], F32, name="dy_tile%d" % j, offset=j * WINDOW, align_bytes=64)
-            nc.sync.dma_start(out=dy_tile[:], in_=dy[j * P : (j + 1) * P, :])
-            dy_tiles.append(dy_tile)
+            windows.append(window)
+        spare = len(sources) * WINDOW
 
         identity = keep.tile([P, P], F32, name="identity")
         make_identity(nc, identity[:])
 
-        def gather_and_turn(window, vector_slots=VECTOR_SLOTS):
-            picked = ring.tile([P, SLOTS], BF16, name="picked", align_bytes=64)
+        def gather_and_turn(n, vector_slots, picked):
             split = vector_slots // 16
-            nc.vector.tensor_copy(picked[:, 0:vector_slots], window[:].indirect(offsets[:, 0:split]))
+            nc.vector.tensor_copy(picked[:, 0:vector_slots], windows[n][:].indirect(offsets[:, 0:split]))
             if vector_slots < SLOTS:
-                nc.scalar.activation(picked[:, vector_slots:SLOTS], window[:].indirect(offsets[:, split:]), COPY)
+                nc.scalar.activation(picked[:, vector_slots:SLOTS], windows[n][:].indirect(offsets[:, split:]), COPY)
             pairs = picked[:].bitcast(F32)
             turned = turn.tile([P, 2, P], F32, name="turned")
             for u in range(2):
                 nc.tensor.transpose(turned[:, u, :], pairs[:, u : 2 * P : 2], identity[:])
             return turned
 
+        def fresh():
+            return ring.tile([P, SLOTS], BF16, name="picked", align_bytes=64)
+
         def group(turned, grouped):
             nc.scalar.copy(
                 out=grouped.bitcast(F32).rearrange("p (m u) -> p m u", u=2), in_=turned.rearrange("p u m -> p m u")
             )
 
-        early = (LANES - 1) * P
-        w_grouped = keep.tile([P, LANES * early], BF16, name="w_grouped", align_bytes=64)
-        for t in range(LANES - 1):
-            group(gather_and_turn(w_tiles[t], SLOTS)[:], w_grouped[:, t * LANES * P : (t + 1) * LANES * P])
-        turned3 = gather_and_turn(w_tiles[LANES - 1], SLOTS)
-        turned = gather_and_turn(dy_tiles[0], SLOTS // 2)
-        w_grouped3 = shared.tile([P, LANES * P], BF16, name="w_grouped3", offset=0, align_bytes=64)
-        group(turned3[:], w_grouped3[:])
-        w_codes = shared.tile([P, D], U32, name="w_codes", offset=WINDOW // 2, align_bytes=64)
-        w_scales = keep.tile([P, D], U8, name="w_scales", align_bytes=64)
-        nc.vector.quantize_mx(out=w_codes[:, 0:early].bitcast(E4M3X4), scales=w_scales[:, 0:early], in_=w_grouped[:])
-        nc.vector.quantize_mx(out=w_codes[:, early:D].bitcast(E4M3X4), scales=w_scales[:, early:D], in_=w_grouped3[:])
-
-        y_scales = keep.tile([P, R], U8, name="y_scales", align_bytes=64)
-
         def multiply(out, t, codes, scales):
-            cols = slice(t * P, (t + 1) * P)
             nc.tensor.matmul_mx(
                 out=out,
-                lhsT=w_codes[:, cols].bitcast(E4M3X4),
-                lhsT_scale=w_scales[:, cols],
-                rhs=codes[:].bitcast(E5M2X4),
-                rhs_scale=scales[:],
+                lhsT=w_codes[t][:].bitcast(E4M3X4),
+                lhsT_scale=w_scales[t][:],
+                rhs=codes.bitcast(E5M2X4),
+                rhs_scale=scales,
                 start=True,
                 stop=True,
             )
 
-        def quantize_and_multiply(turned):
-            grouped = ring.tile([P, LANES * P], BF16, name="grouped", align_bytes=64)
-            codes = ring.tile([P, P], U32, name="codes", align_bytes=64)
-            scales = ring.tile([P, P], U8, name="scales", align_bytes=64)
-            for rows in (slice(0, P // 2), slice(P // 2, P)):
-                group(turned[:, :, rows], grouped[:, LANES * rows.start : LANES * rows.stop])
-            for rows in (slice(0, P // 2), slice(P // 2, P)):
+        def multiply_early(t):
+            bank = sums.tile([P, early], F32, name="bank")
+            for cols in (slice(0, 2 * P), slice(2 * P, early)):
+                multiply(bank[:, cols], t, dy_codes[:, cols], dy_scales[:, cols])
+            return bank
+
+        def quantize_lane(t, codes, grouped, pieces):
+            scales = keep.tile([P, P], U8, name="w_scales%d" % t, align_bytes=64)
+            width = P // pieces
+            for h in range(pieces):
+                rows = slice(h * width, (h + 1) * width)
                 nc.vector.quantize_mx(
-                    out=codes[:, rows].bitcast(E5M2X4),
+                    out=codes[:, rows].bitcast(E4M3X4),
                     scales=scales[:, rows],
                     in_=grouped[:, LANES * rows.start : LANES * rows.stop],
                 )
-            bank = sums.tile([P, LANES, P], F32, name="bank")
-            for t in range(LANES):
-                multiply(bank[:, t, :], t, codes, scales)
-            return bank
+            w_codes.append(codes)
+            w_scales.append(scales)
 
-        def quantize_result(j, codes, rounded):
+        def quantize_result(cols, codes, rounded):
             nc.vector.quantize_mx(
-                out=codes.bitcast(E4M3X4),
-                scales=y_scales[:, j * P : (j + 1) * P],
-                in_=rounded[:].rearrange("p r t -> p (r t)"),
+                out=codes.bitcast(E4M3X4), scales=y_scales[:, cols], in_=rounded[:].rearrange("p r t -> p (r t)")
             )
 
-        def round_sums(j, bank):
-            rounded = shared.tile([P, P, LANES], BF16, name="rounded%d" % j, offset=(j + 1) * WINDOW, align_bytes=64)
-            nc.vector.tensor_copy(out=rounded[:], in_=bank[:].rearrange("p t r -> p r t"))
-            return rounded
-
-        def hand_out(j, bank, rounded):
-            base = (j + 2) * WINDOW
-            codes = shared.tile([P, P], U32, name="y_codes%d" % j, offset=base + WINDOW // 4, align_bytes=64)
-            quantize_result(j, codes[:], rounded)
-            y = shared.tile([P, LANES, P], F32, name="y%d" % j, offset=base + WINDOW // 2, align_bytes=64)
-            nc.scalar.copy(out=y[:], in_=bank[:])
-            nc.sync.dma_start(out=out_words[:, j * P : (j + 1) * P], in_=codes[:].bitcast(I32))
-            nc.sync.dma_start(out=out_rows[:, :, j * P : (j + 1) * P], in_=y[:])
-
-        bank0 = quantize_and_multiply(turned)
-
-        turned = gather_and_turn(dy_tiles[1])
-        rounded0 = round_sums(0, bank0)
-        bank1 = quantize_and_multiply(turned)
-
-        turned = gather_and_turn(dy_tiles[2])
-        hand_out(0, bank0, rounded0)
-        rounded1 = round_sums(1, bank1)
-        bank2 = quantize_and_multiply(turned)
-
-        last = TILES - 1
-        turned = gather_and_turn(dy_tiles[last])
-        hand_out(1, bank1, rounded1)
-        rounded2 = round_sums(2, bank2)
+        w_codes = []
+        w_scales = []
+        y_scales = keep.tile([P, R], U8, name="y_scales", align_bytes=64)
         half = P // 2
-        first_half = shared.tile([P, LANES * half], BF16, name="first_half", offset=4 * WINDOW + 768, align_bytes=64)
+        halves = [slice(0, half), slice(half, P)]
+
+        dy_grouped = keep.tile([P, LANES * early], BF16, name="dy_grouped", align_bytes=64)
+        for j in range(last):
+            group(gather_and_turn(j, SLOTS, fresh())[:], dy_grouped[:, j * LANES * P : (j + 1) * LANES * P])
+        w_grouped = [keep.tile([P, LANES * P], BF16, name="w_grouped%d" % t, align_bytes=64) for t in range(2)]
+        group(gather_and_turn(last, SLOTS, fresh())[:], w_grouped[0][:])
+        dy_codes = shared.tile([P, early], U32, name="dy_codes", offset=last * WINDOW, align_bytes=64)
+        dy_scales = keep.tile([P, early], U8, name="dy_scales", align_bytes=64)
+        for cols in (slice(0, 2 * P), slice(2 * P, early)):
+            nc.vector.quantize_mx(
+                out=dy_codes[:, cols].bitcast(E5M2X4),
+                scales=dy_scales[:, cols],
+                in_=dy_grouped[:, LANES * cols.start : LANES * cols.stop],
+            )
+
+        picked1 = shared.tile([P, SLOTS], BF16, name="picked1", offset=spare, align_bytes=64)
+        group(gather_and_turn(last + 1, SLOTS, picked1)[:], w_grouped[1][:])
+        y01 = keep.tile([P, 2, early], F32, name="y01", align_bytes=64)
+        quantize_lane(0, shared.tile([P, P], U32, name="w_codes0", offset=spare, align_bytes=64), w_grouped[0], 1)
+        nc.scalar.copy(out=y01[:, 0, :], in_=multiply_early(0)[:])
+        quantize_lane(1, keep.tile([P, P], U32, name="w_codes1", align_bytes=64), w_grouped[1], 1)
+        nc.scalar.copy(out=y01[:, 1, :], in_=multiply_early(1)[:])
+        nc.sync.dma_start(out=out_rows[:, 0:2, 0:early], in_=y01[:])
+
+        turned2 = gather_and_turn(last + 2, SLOTS, fresh())
+        turned3 = gather_and_turn(last + 3, SLOTS // 2, fresh())
+        base = (last + 3) * WINDOW
+        w_grouped2 = shared.tile([P, LANES * P], BF16, name="w_grouped2", offset=base, align_bytes=64)
+        group(turned2[:], w_grouped2[:])
+        rounded_a = shared.tile([P, 2 * P, LANES], BF16, name="rounded_a", offset=base + WINDOW // 2, align_bytes=64)
+        nc.vector.tensor_copy(out=rounded_a[:, :, 0:2], in_=y01[:, :, 0 : 2 * P].rearrange("p t r -> p r t"))
+        quantize_lane(2, keep.tile([P, P], U32, name="w_codes2", align_bytes=64), w_grouped2, 1)
+        bank2 = multiply_early(2)
+        w_grouped3 = keep.tile([P, LANES * P], BF16, name="w_grouped3", align_bytes=64)
+        for rows in halves:
+            group(turned3[:, :, rows], w_grouped3[:, LANES * rows.start : LANES * rows.stop])
+        quantize_lane(3, keep.tile([P, P], U32, name="w_codes3", align_bytes=64), w_grouped3, 2)
+        bank3 = multiply_early(3)
+
+        turned = gather_and_turn(last + LANES, VECTOR_SLOTS, fresh())
+        y23 = shared.tile([P, 2, early], F32, name="y23", offset=(last + LANES) * WINDOW, align_bytes=64)
+        nc.vector.tensor_copy(out=y23[:, 0, :], in_=bank2[:])
+        for j in range(last):
+            nc.scalar.copy(out=y23[:, 1, j * P : (j + 1) * P], in_=bank3[:, j * P : (j + 1) * P])
+        nc.sync.dma_start(out=out_rows[:, 2:4, 0:early], in_=y23[:])
+        for j in range(2):
+            cols = slice(j * P, (j + 1) * P)
+            nc.vector.tensor_copy(out=rounded_a[:, cols, 2:4], in_=y23[:, :, cols].rearrange("p t r -> p r t"))
+
+        held = spare + 2 * SLOTS
+        first_half = shared.tile([P, LANES * half], BF16, name="first_half", offset=held + 768, align_bytes=64)
         second_half = keep.tile([P, LANES * half], BF16, name="second_half", align_bytes=64)
         codes = keep.tile([P, P], U32, name="last_codes", align_bytes=64)
         scales = keep.tile([P, P], U8, name="last_scales", align_bytes=64)
-        halves = [(slice(0, half), first_half), (slice(half, P), second_half)]
-        for rows, grouped in halves:
+        for rows, grouped in zip(halves, (first_half, second_half)):
             group(turned[:, :, rows], grouped[:])
-        for rows, grouped in halves:
+        for rows, grouped in zip(halves, (first_half, second_half)):
             nc.vector.quantize_mx(out=codes[:, rows].bitcast(E5M2X4), scales=scales[:, rows], in_=grouped[:])
         low = ends.tile([P, 2, P], F32, name="low")
         high = ends.tile([P, 2, P], F32, name="high")
         for t in range(LANES):
-            multiply((low, high)[t // 2][:, t % 2, :], t, codes, scales)
+            multiply((low, high)[t // 2][:, t % 2, :], t, codes[:], scales[:])
 
-        y2 = shared.tile([P, LANES, P], F32, name="y2", offset=4 * WINDOW + 1024, align_bytes=64)
-        nc.scalar.copy(out=y2[:], in_=bank2[:])
-        nc.sync.dma_start(out=out_rows[:, :, 2 * P : 3 * P], in_=y2[:])
-        codes23 = shared.tile([P, 2 * P], U32, name="y_codes23", offset=4 * WINDOW, align_bytes=64)
-        quantize_result(2, codes23[:, 0:P], rounded2)
+        rounded_c = shared.tile([P, P, LANES], BF16, name="rounded_c", offset=held + 1024, align_bytes=64)
+        third = slice(2 * P, early)
+        nc.scalar.copy(out=rounded_c[:, :, 2:4], in_=y23[:, :, third].rearrange("p t r -> p r t"))
+        nc.vector.tensor_copy(out=rounded_c[:, :, 0:2], in_=y01[:, :, third].rearrange("p t r -> p r t"))
+        codes_a = shared.tile([P, 2 * P], U32, name="y_codes_a", offset=held, align_bytes=64)
+        quantize_result(slice(0, 2 * P), codes_a[:], rounded_a)
+        nc.sync.dma_start(out=out_words[:, 0 : 2 * P], in_=codes_a[:].bitcast(I32))
+        codes_b = keep.tile([P, 2 * P], U32, name="y_codes_b", align_bytes=64)
+        quantize_result(third, codes_b[:, 0:P], rounded_c)
 
         rounded = keep.tile([P, P, LANES], BF16, name="last_rounded", align_bytes=64)
         y_low = keep.tile([P, 2, P], F32, name="y_low", align_bytes=64)
         y_high = keep.tile([P, 2, P], F32, name="y_high", align_bytes=64)
+        nc.vector.tensor_copy(out=y_low[:], in_=low[:])
+        nc.sync.dma_start(out=out_rows[:, 0:2, early:R], in_=y_low[:])
         nc.vector.tensor_copy(out=rounded[:, :, 0:2], in_=low[:].rearrange("p t r -> p r t"))
         nc.scalar.copy(out=rounded[:, :, 2:4], in_=high[:].rearrange("p t r -> p r t"))
-        nc.vector.tensor_copy(out=y_low[:], in_=low[:])
         nc.scalar.copy(out=y_high[:], in_=high[:])
-        quantize_result(last, codes23[:, P : 2 * P], rounded)
-        nc.sync.dma_start(out=out_rows[:, 0:2, last * P : R], in_=y_low[:])
-        nc.scalar.dma_start(out=out_rows[:, 2:4, last * P : R], in_=y_high[:])
-        nc.sync.dma_start(out=out_words[:, 2 * P : R], in_=codes23[:].bitcast(I32))
+        quantize_result(slice(early, R), codes_b[:, P : 2 * P], rounded)
+        nc.scalar.dma_start(out=out_rows[:, 2:4, early:R], in_=y_high[:])
+        nc.sync.dma_start(out=out_words[:, 2 * P : R], in_=codes_b[:].bitcast(I32))
         for g in range(P // 32):
             queue = nc.scalar if g % 2 == 0 else nc.sync
             queue.dma_start(

@@ -20,7 +20,7 @@ R = 512
 SLOTS = 512
 UNITS = 2048
 TILES = R // P
-VECTOR_SLOTS = 192
+VECTOR_SLOTS = 224
 WINDOW = 4 * UNITS
 
 FLOPS = 2 * D * R * SLOTS
@@ -37,23 +37,25 @@ def tile_attend_gmeprop_x_pl_kernel(tc, dy, wT, offs, out_0, out_1, out_2):
         keep = ctx.enter_context(tc.tile_pool(name="keep", bufs=1))
         ring = ctx.enter_context(tc.tile_pool(name="ring", bufs=2))
         shared = ctx.enter_context(tc.tile_pool(name="shared", bufs=1))
-        turn = ctx.enter_context(tc.psum_pool(name="turn", bufs=3))
+        turn = ctx.enter_context(tc.psum_pool(name="turn", bufs=2))
         sums = ctx.enter_context(tc.psum_pool(name="sums", bufs=2))
         ends = ctx.enter_context(tc.psum_pool(name="ends", bufs=1))
 
         offsets = keep.tile([P, SLOTS // 16], U16, name="offsets")
         last = TILES - 1
         early = last * P
-        sources = [dy[j * P : (j + 1) * P, :] for j in range(last)] + [w_rows[:, t, :] for t in range(LANES)]
-        sources.append(dy[early:R, :])
-        windows = []
-        for n, source in enumerate(sources):
-            window = shared.tile([P, UNITS], F32, name="window%d" % n, offset=n * WINDOW, align_bytes=64)
-            nc.sync.dma_start(out=window[:], in_=source)
-            if n == 0:
-                nc.sync.dma_start(offsets[:], offs)
-            windows.append(window)
-        spare = len(sources) * WINDOW
+        dy_pair = keep.tile([P, 2, UNITS], F32, name="dy_pair", align_bytes=64)
+        nc.sync.dma_start(out=dy_pair[:], in_=dy[0 : 2 * P, :].rearrange("(j p) k -> p j k", j=2))
+        nc.sync.dma_start(offsets[:], offs)
+        sources = {2: dy[2 * P : early, :]}
+        for t in range(LANES):
+            sources[last + t] = w_rows[:, t, :]
+        sources[last + LANES] = dy[early:R, :]
+        windows = {}
+        for n in sorted(sources):
+            windows[n] = shared.tile([P, UNITS], F32, name="window%d" % n, offset=n * WINDOW, align_bytes=64)
+            nc.sync.dma_start(out=windows[n][:], in_=sources[n])
+        spare = (last + LANES + 1) * WINDOW
 
         identity = keep.tile([P, P], F32, name="identity")
         make_identity(nc, identity[:])
@@ -119,8 +121,16 @@ def tile_attend_gmeprop_x_pl_kernel(tc, dy, wT, offs, out_0, out_1, out_2):
         halves = [slice(0, half), slice(half, P)]
 
         dy_grouped = keep.tile([P, LANES * early], BF16, name="dy_grouped", align_bytes=64)
-        for j in range(last):
-            group(gather_and_turn(j, SLOTS, fresh())[:], dy_grouped[:, j * LANES * P : (j + 1) * LANES * P])
+        for j in range(2):
+            picked = fresh()
+            nc.vector.tensor_copy(
+                picked[:].rearrange("p (u s c) -> p s u c", u=2, c=2), dy_pair[:, j, :].indirect(offsets[:])
+            )
+            turned = turn.tile([P, 2, P], F32, name="turned")
+            for u in range(2):
+                nc.tensor.transpose(turned[:, u, :], picked[:].bitcast(F32)[:, u * P : (u + 1) * P], identity[:])
+            group(turned[:], dy_grouped[:, j * LANES * P : (j + 1) * LANES * P])
+        group(gather_and_turn(2, SLOTS, fresh())[:], dy_grouped[:, 2 * LANES * P : last * LANES * P])
         w_grouped = [keep.tile([P, LANES * P], BF16, name="w_grouped%d" % t, align_bytes=64) for t in range(2)]
         group(gather_and_turn(last, SLOTS, fresh())[:], w_grouped[0][:])
         dy_codes = shared.tile([P, early], U32, name="dy_codes", offset=last * WINDOW, align_bytes=64)
@@ -149,24 +159,29 @@ def tile_attend_gmeprop_x_pl_kernel(tc, dy, wT, offs, out_0, out_1, out_2):
         rounded_a = shared.tile([P, 2 * P, LANES], BF16, name="rounded_a", offset=base + WINDOW // 2, align_bytes=64)
         nc.vector.tensor_copy(out=rounded_a[:, :, 0:2], in_=y01[:, :, 0 : 2 * P].rearrange("p t r -> p r t"))
         quantize_lane(2, keep.tile([P, P], U32, name="w_codes2", align_bytes=64), w_grouped2, 1)
-        bank2 = multiply_early(2)
+        wide = ends.tile([P, 2, 2 * P], F32, name="wide")
+        narrow = ends.tile([P, 2, P], F32, name="narrow")
+        third = slice(2 * P, early)
+        multiply(wide[:, 0, :], 2, dy_codes[:, 0 : 2 * P], dy_scales[:, 0 : 2 * P])
+        multiply(narrow[:, 0, :], 2, dy_codes[:, third], dy_scales[:, third])
         w_grouped3 = keep.tile([P, LANES * P], BF16, name="w_grouped3", align_bytes=64)
         for rows in halves:
             group(turned3[:, :, rows], w_grouped3[:, LANES * rows.start : LANES * rows.stop])
         quantize_lane(3, keep.tile([P, P], U32, name="w_codes3", align_bytes=64), w_grouped3, 2)
-        bank3 = multiply_early(3)
+        multiply(wide[:, 1, :], 3, dy_codes[:, 0 : 2 * P], dy_scales[:, 0 : 2 * P])
+        multiply(narrow[:, 1, :], 3, dy_codes[:, third], dy_scales[:, third])
 
         turned = gather_and_turn(last + LANES, VECTOR_SLOTS, fresh())
         y23 = shared.tile([P, 2, early], F32, name="y23", offset=(last + LANES) * WINDOW, align_bytes=64)
-        nc.vector.tensor_copy(out=y23[:, 0, :], in_=bank2[:])
-        for j in range(last):
-            nc.scalar.copy(out=y23[:, 1, j * P : (j + 1) * P], in_=bank3[:, j * P : (j + 1) * P])
+        for j in range(2):
+            nc.scalar.copy(out=y23[:, :, j * P : (j + 1) * P], in_=wide[:, :, j * P : (j + 1) * P])
+        nc.vector.tensor_copy(out=y23[:, :, third], in_=narrow[:])
         nc.sync.dma_start(out=out_rows[:, 2:4, 0:early], in_=y23[:])
         for j in range(2):
             cols = slice(j * P, (j + 1) * P)
             nc.vector.tensor_copy(out=rounded_a[:, cols, 2:4], in_=y23[:, :, cols].rearrange("p t r -> p r t"))
 
-        held = spare + 2 * SLOTS
+        held = spare + 4 * SLOTS
         first_half = shared.tile([P, LANES * half], BF16, name="first_half", offset=held + 768, align_bytes=64)
         second_half = keep.tile([P, LANES * half], BF16, name="second_half", align_bytes=64)
         codes = keep.tile([P, P], U32, name="last_codes", align_bytes=64)
@@ -181,14 +196,13 @@ def tile_attend_gmeprop_x_pl_kernel(tc, dy, wT, offs, out_0, out_1, out_2):
             multiply((low, high)[t // 2][:, t % 2, :], t, codes[:], scales[:])
 
         rounded_c = shared.tile([P, P, LANES], BF16, name="rounded_c", offset=held + 1024, align_bytes=64)
-        third = slice(2 * P, early)
         nc.scalar.copy(out=rounded_c[:, :, 2:4], in_=y23[:, :, third].rearrange("p t r -> p r t"))
         nc.vector.tensor_copy(out=rounded_c[:, :, 0:2], in_=y01[:, :, third].rearrange("p t r -> p r t"))
-        codes_a = shared.tile([P, 2 * P], U32, name="y_codes_a", offset=held, align_bytes=64)
-        quantize_result(slice(0, 2 * P), codes_a[:], rounded_a)
-        nc.sync.dma_start(out=out_words[:, 0 : 2 * P], in_=codes_a[:].bitcast(I32))
-        codes_b = keep.tile([P, 2 * P], U32, name="y_codes_b", align_bytes=64)
-        quantize_result(third, codes_b[:, 0:P], rounded_c)
+        codes_a = shared.tile([P, early], U32, name="y_codes_a", offset=held - 512, align_bytes=64)
+        quantize_result(slice(0, 2 * P), codes_a[:, 0 : 2 * P], rounded_a)
+        quantize_result(third, codes_a[:, third], rounded_c)
+        nc.sync.dma_start(out=out_words[:, 0:early], in_=codes_a[:].bitcast(I32))
+        codes_b = keep.tile([P, P], U32, name="y_codes_b", align_bytes=64)
 
         rounded = keep.tile([P, P, LANES], BF16, name="last_rounded", align_bytes=64)
         y_low = keep.tile([P, 2, P], F32, name="y_low", align_bytes=64)
@@ -198,9 +212,9 @@ def tile_attend_gmeprop_x_pl_kernel(tc, dy, wT, offs, out_0, out_1, out_2):
         nc.vector.tensor_copy(out=rounded[:, :, 0:2], in_=low[:].rearrange("p t r -> p r t"))
         nc.scalar.copy(out=rounded[:, :, 2:4], in_=high[:].rearrange("p t r -> p r t"))
         nc.scalar.copy(out=y_high[:], in_=high[:])
-        quantize_result(slice(early, R), codes_b[:, P : 2 * P], rounded)
-        nc.scalar.dma_start(out=out_rows[:, 2:4, early:R], in_=y_high[:])
-        nc.sync.dma_start(out=out_words[:, 2 * P : R], in_=codes_b[:].bitcast(I32))
+        nc.sync.dma_start(out=out_rows[:, 2:4, early:R], in_=y_high[:])
+        quantize_result(slice(early, R), codes_b[:], rounded)
+        nc.sync.dma_start(out=out_words[:, early:R], in_=codes_b[:].bitcast(I32))
         for g in range(P // 32):
             queue = nc.scalar if g % 2 == 0 else nc.sync
             queue.dma_start(

@@ -19,9 +19,19 @@ D = 512
 R = 512
 SLOTS = 512
 UNITS = 2048
-TILES = R // P
-VECTOR_SLOTS = 224
 WINDOW = 4 * UNITS
+PAIR = slice(0, 2 * P)
+THIRD = slice(2 * P, 3 * P)
+EARLY = slice(0, 3 * P)
+LAST = slice(3 * P, R)
+DY2 = 2
+LANE0 = 3
+DY3 = LANE0 + LANES
+LAST_VECTOR_SLOTS = 224
+AFTER_WINDOWS = (DY3 + 1) * WINDOW
+EARLY_CODES = AFTER_WINDOWS + 1536
+FIRST_HALF = EARLY_CODES + 1536 - 256
+ROUNDED_THIRD = FIRST_HALF + 256
 
 FLOPS = 2 * D * R * SLOTS
 
@@ -42,20 +52,14 @@ def tile_attend_gmeprop_x_pl_kernel(tc, dy, wT, offs, out_0, out_1, out_2):
         ends = ctx.enter_context(tc.psum_pool(name="ends", bufs=1))
 
         offsets = keep.tile([P, SLOTS // 16], U16, name="offsets")
-        last = TILES - 1
-        early = last * P
         dy_pair = keep.tile([P, 2, UNITS], F32, name="dy_pair", align_bytes=64)
-        nc.sync.dma_start(out=dy_pair[:], in_=dy[0 : 2 * P, :].rearrange("(j p) k -> p j k", j=2))
+        nc.sync.dma_start(out=dy_pair[:], in_=dy[PAIR, :].rearrange("(j p) k -> p j k", j=2))
         nc.sync.dma_start(offsets[:], offs)
-        sources = {2: dy[2 * P : early, :]}
-        for t in range(LANES):
-            sources[last + t] = w_rows[:, t, :]
-        sources[last + LANES] = dy[early:R, :]
+        sources = [dy[THIRD, :]] + [w_rows[:, t, :] for t in range(LANES)] + [dy[LAST, :]]
         windows = {}
-        for n in sorted(sources):
+        for n, source in enumerate(sources, DY2):
             windows[n] = shared.tile([P, UNITS], F32, name="window%d" % n, offset=n * WINDOW, align_bytes=64)
-            nc.sync.dma_start(out=windows[n][:], in_=sources[n])
-        spare = (last + LANES + 1) * WINDOW
+            nc.sync.dma_start(out=windows[n][:], in_=source)
 
         identity = keep.tile([P, P], F32, name="identity")
         make_identity(nc, identity[:])
@@ -65,19 +69,22 @@ def tile_attend_gmeprop_x_pl_kernel(tc, dy, wT, offs, out_0, out_1, out_2):
             nc.vector.tensor_copy(picked[:, 0:vector_slots], windows[n][:].indirect(offsets[:, 0:split]))
             if vector_slots < SLOTS:
                 nc.scalar.activation(picked[:, vector_slots:SLOTS], windows[n][:].indirect(offsets[:, split:]), COPY)
-            pairs = picked[:].bitcast(F32)
+            words = picked[:].bitcast(F32)
             turned = turn.tile([P, 2, P], F32, name="turned")
             for u in range(2):
-                nc.tensor.transpose(turned[:, u, :], pairs[:, u : 2 * P : 2], identity[:])
+                nc.tensor.transpose(turned[:, u, :], words[:, u : 2 * P : 2], identity[:])
             return turned
 
-        def fresh():
+        def picked_tile():
             return ring.tile([P, SLOTS], BF16, name="picked", align_bytes=64)
 
         def group(turned, grouped):
             nc.scalar.copy(
                 out=grouped.bitcast(F32).rearrange("p (m u) -> p m u", u=2), in_=turned.rearrange("p u m -> p m u")
             )
+
+        def values(cols):
+            return slice(LANES * cols.start, LANES * cols.stop)
 
         def multiply(out, t, codes, scales):
             nc.tensor.matmul_mx(
@@ -91,20 +98,16 @@ def tile_attend_gmeprop_x_pl_kernel(tc, dy, wT, offs, out_0, out_1, out_2):
             )
 
         def multiply_early(t):
-            bank = sums.tile([P, early], F32, name="bank")
-            for cols in (slice(0, 2 * P), slice(2 * P, early)):
+            bank = sums.tile([P, EARLY.stop], F32, name="bank")
+            for cols in (PAIR, THIRD):
                 multiply(bank[:, cols], t, dy_codes[:, cols], dy_scales[:, cols])
             return bank
 
         def quantize_lane(t, codes, grouped, pieces):
             scales = keep.tile([P, P], U8, name="w_scales%d" % t, align_bytes=64)
-            width = P // pieces
-            for h in range(pieces):
-                rows = slice(h * width, (h + 1) * width)
+            for rows in pieces:
                 nc.vector.quantize_mx(
-                    out=codes[:, rows].bitcast(E4M3X4),
-                    scales=scales[:, rows],
-                    in_=grouped[:, LANES * rows.start : LANES * rows.stop],
+                    out=codes[:, rows].bitcast(E4M3X4), scales=scales[:, rows], in_=grouped[:, values(rows)]
                 )
             w_codes.append(codes)
             w_scales.append(scales)
@@ -117,104 +120,103 @@ def tile_attend_gmeprop_x_pl_kernel(tc, dy, wT, offs, out_0, out_1, out_2):
         w_codes = []
         w_scales = []
         y_scales = keep.tile([P, R], U8, name="y_scales", align_bytes=64)
-        half = P // 2
-        halves = [slice(0, half), slice(half, P)]
+        whole = [slice(0, P)]
+        halves = [slice(0, P // 2), slice(P // 2, P)]
 
-        dy_grouped = keep.tile([P, LANES * early], BF16, name="dy_grouped", align_bytes=64)
+        dy_grouped = keep.tile([P, LANES * EARLY.stop], BF16, name="dy_grouped", align_bytes=64)
         for j in range(2):
-            picked = fresh()
+            picked = picked_tile()
             nc.vector.tensor_copy(
                 picked[:].rearrange("p (u s c) -> p s u c", u=2, c=2), dy_pair[:, j, :].indirect(offsets[:])
             )
             turned = turn.tile([P, 2, P], F32, name="turned")
             for u in range(2):
                 nc.tensor.transpose(turned[:, u, :], picked[:].bitcast(F32)[:, u * P : (u + 1) * P], identity[:])
-            group(turned[:], dy_grouped[:, j * LANES * P : (j + 1) * LANES * P])
-        group(gather_and_turn(2, SLOTS, fresh())[:], dy_grouped[:, 2 * LANES * P : last * LANES * P])
+            group(turned[:], dy_grouped[:, values(slice(j * P, (j + 1) * P))])
+        group(gather_and_turn(DY2, SLOTS, picked_tile())[:], dy_grouped[:, values(THIRD)])
         w_grouped = [keep.tile([P, LANES * P], BF16, name="w_grouped%d" % t, align_bytes=64) for t in range(2)]
-        group(gather_and_turn(last, SLOTS, fresh())[:], w_grouped[0][:])
-        dy_codes = shared.tile([P, early], U32, name="dy_codes", offset=last * WINDOW, align_bytes=64)
-        dy_scales = keep.tile([P, early], U8, name="dy_scales", align_bytes=64)
-        for cols in (slice(0, 2 * P), slice(2 * P, early)):
+        group(gather_and_turn(LANE0, SLOTS, picked_tile())[:], w_grouped[0][:])
+        dy_codes = shared.tile([P, EARLY.stop], U32, name="dy_codes", offset=LANE0 * WINDOW, align_bytes=64)
+        dy_scales = keep.tile([P, EARLY.stop], U8, name="dy_scales", align_bytes=64)
+        for cols in (PAIR, THIRD):
             nc.vector.quantize_mx(
-                out=dy_codes[:, cols].bitcast(E5M2X4),
-                scales=dy_scales[:, cols],
-                in_=dy_grouped[:, LANES * cols.start : LANES * cols.stop],
+                out=dy_codes[:, cols].bitcast(E5M2X4), scales=dy_scales[:, cols], in_=dy_grouped[:, values(cols)]
             )
 
-        picked1 = shared.tile([P, SLOTS], BF16, name="picked1", offset=spare, align_bytes=64)
-        group(gather_and_turn(last + 1, SLOTS, picked1)[:], w_grouped[1][:])
-        y01 = keep.tile([P, 2, early], F32, name="y01", align_bytes=64)
-        quantize_lane(0, shared.tile([P, P], U32, name="w_codes0", offset=spare, align_bytes=64), w_grouped[0], 1)
+        picked1 = shared.tile([P, SLOTS], BF16, name="picked1", offset=AFTER_WINDOWS, align_bytes=64)
+        group(gather_and_turn(LANE0 + 1, SLOTS, picked1)[:], w_grouped[1][:])
+        y01 = keep.tile([P, 2, EARLY.stop], F32, name="y01", align_bytes=64)
+        w_codes0 = shared.tile([P, P], U32, name="w_codes0", offset=AFTER_WINDOWS, align_bytes=64)
+        quantize_lane(0, w_codes0, w_grouped[0], whole)
         nc.scalar.copy(out=y01[:, 0, :], in_=multiply_early(0)[:])
-        quantize_lane(1, keep.tile([P, P], U32, name="w_codes1", align_bytes=64), w_grouped[1], 1)
+        quantize_lane(1, keep.tile([P, P], U32, name="w_codes1", align_bytes=64), w_grouped[1], whole)
         nc.scalar.copy(out=y01[:, 1, :], in_=multiply_early(1)[:])
-        nc.sync.dma_start(out=out_rows[:, 0:2, 0:early], in_=y01[:])
+        nc.sync.dma_start(out=out_rows[:, 0:2, EARLY], in_=y01[:])
 
-        turned2 = gather_and_turn(last + 2, SLOTS, fresh())
-        turned3 = gather_and_turn(last + 3, SLOTS // 2, fresh())
-        base = (last + 3) * WINDOW
-        w_grouped2 = shared.tile([P, LANES * P], BF16, name="w_grouped2", offset=base, align_bytes=64)
+        turned2 = gather_and_turn(LANE0 + 2, SLOTS, picked_tile())
+        turned3 = gather_and_turn(LANE0 + 3, SLOTS // 2, picked_tile())
+        lane3_bytes = (LANE0 + 3) * WINDOW
+        w_grouped2 = shared.tile([P, LANES * P], BF16, name="w_grouped2", offset=lane3_bytes, align_bytes=64)
         group(turned2[:], w_grouped2[:])
-        rounded_a = shared.tile([P, 2 * P, LANES], BF16, name="rounded_a", offset=base + WINDOW // 2, align_bytes=64)
-        nc.vector.tensor_copy(out=rounded_a[:, :, 0:2], in_=y01[:, :, 0 : 2 * P].rearrange("p t r -> p r t"))
-        quantize_lane(2, keep.tile([P, P], U32, name="w_codes2", align_bytes=64), w_grouped2, 1)
-        wide = ends.tile([P, 2, 2 * P], F32, name="wide")
-        narrow = ends.tile([P, 2, P], F32, name="narrow")
-        third = slice(2 * P, early)
-        multiply(wide[:, 0, :], 2, dy_codes[:, 0 : 2 * P], dy_scales[:, 0 : 2 * P])
-        multiply(narrow[:, 0, :], 2, dy_codes[:, third], dy_scales[:, third])
+        rounded_pair = shared.tile(
+            [P, PAIR.stop, LANES], BF16, name="rounded_pair", offset=lane3_bytes + WINDOW // 2, align_bytes=64
+        )
+        nc.vector.tensor_copy(out=rounded_pair[:, :, 0:2], in_=y01[:, :, PAIR].rearrange("p t r -> p r t"))
+        quantize_lane(2, keep.tile([P, P], U32, name="w_codes2", align_bytes=64), w_grouped2, whole)
+        pair_bank = ends.tile([P, 2, PAIR.stop], F32, name="pair_bank")
+        third_bank = ends.tile([P, 2, P], F32, name="third_bank")
+        multiply(pair_bank[:, 0, :], 2, dy_codes[:, PAIR], dy_scales[:, PAIR])
+        multiply(third_bank[:, 0, :], 2, dy_codes[:, THIRD], dy_scales[:, THIRD])
         w_grouped3 = keep.tile([P, LANES * P], BF16, name="w_grouped3", align_bytes=64)
         for rows in halves:
-            group(turned3[:, :, rows], w_grouped3[:, LANES * rows.start : LANES * rows.stop])
-        quantize_lane(3, keep.tile([P, P], U32, name="w_codes3", align_bytes=64), w_grouped3, 2)
-        multiply(wide[:, 1, :], 3, dy_codes[:, 0 : 2 * P], dy_scales[:, 0 : 2 * P])
-        multiply(narrow[:, 1, :], 3, dy_codes[:, third], dy_scales[:, third])
+            group(turned3[:, :, rows], w_grouped3[:, values(rows)])
+        quantize_lane(3, keep.tile([P, P], U32, name="w_codes3", align_bytes=64), w_grouped3, halves)
+        multiply(pair_bank[:, 1, :], 3, dy_codes[:, PAIR], dy_scales[:, PAIR])
+        multiply(third_bank[:, 1, :], 3, dy_codes[:, THIRD], dy_scales[:, THIRD])
 
-        turned = gather_and_turn(last + LANES, VECTOR_SLOTS, fresh())
-        y23 = shared.tile([P, 2, early], F32, name="y23", offset=(last + LANES) * WINDOW, align_bytes=64)
-        for j in range(2):
-            nc.scalar.copy(out=y23[:, :, j * P : (j + 1) * P], in_=wide[:, :, j * P : (j + 1) * P])
-        nc.vector.tensor_copy(out=y23[:, :, third], in_=narrow[:])
-        nc.sync.dma_start(out=out_rows[:, 2:4, 0:early], in_=y23[:])
-        for j in range(2):
-            cols = slice(j * P, (j + 1) * P)
-            nc.vector.tensor_copy(out=rounded_a[:, cols, 2:4], in_=y23[:, :, cols].rearrange("p t r -> p r t"))
+        turned = gather_and_turn(DY3, LAST_VECTOR_SLOTS, picked_tile())
+        y23 = shared.tile([P, 2, EARLY.stop], F32, name="y23", offset=DY3 * WINDOW, align_bytes=64)
+        pair_tiles = [slice(j * P, (j + 1) * P) for j in range(2)]
+        for cols in pair_tiles:
+            nc.scalar.copy(out=y23[:, :, cols], in_=pair_bank[:, :, cols])
+        nc.vector.tensor_copy(out=y23[:, :, THIRD], in_=third_bank[:])
+        nc.sync.dma_start(out=out_rows[:, 2:4, EARLY], in_=y23[:])
+        for cols in pair_tiles:
+            nc.vector.tensor_copy(out=rounded_pair[:, cols, 2:4], in_=y23[:, :, cols].rearrange("p t r -> p r t"))
 
-        held = spare + 4 * SLOTS
-        first_half = shared.tile([P, LANES * half], BF16, name="first_half", offset=held + 768, align_bytes=64)
-        second_half = keep.tile([P, LANES * half], BF16, name="second_half", align_bytes=64)
-        codes = keep.tile([P, P], U32, name="last_codes", align_bytes=64)
-        scales = keep.tile([P, P], U8, name="last_scales", align_bytes=64)
+        first_half = shared.tile([P, LANES * P // 2], BF16, name="first_half", offset=FIRST_HALF, align_bytes=64)
+        second_half = keep.tile([P, LANES * P // 2], BF16, name="second_half", align_bytes=64)
+        last_codes = keep.tile([P, P], U32, name="last_codes", align_bytes=64)
+        last_scales = keep.tile([P, P], U8, name="last_scales", align_bytes=64)
         for rows, grouped in zip(halves, (first_half, second_half)):
             group(turned[:, :, rows], grouped[:])
         for rows, grouped in zip(halves, (first_half, second_half)):
-            nc.vector.quantize_mx(out=codes[:, rows].bitcast(E5M2X4), scales=scales[:, rows], in_=grouped[:])
+            nc.vector.quantize_mx(out=last_codes[:, rows].bitcast(E5M2X4), scales=last_scales[:, rows], in_=grouped[:])
         low = ends.tile([P, 2, P], F32, name="low")
         high = ends.tile([P, 2, P], F32, name="high")
         for t in range(LANES):
-            multiply((low, high)[t // 2][:, t % 2, :], t, codes[:], scales[:])
+            multiply((low, high)[t // 2][:, t % 2, :], t, last_codes[:], last_scales[:])
 
-        rounded_c = shared.tile([P, P, LANES], BF16, name="rounded_c", offset=held + 1024, align_bytes=64)
-        nc.scalar.copy(out=rounded_c[:, :, 2:4], in_=y23[:, :, third].rearrange("p t r -> p r t"))
-        nc.vector.tensor_copy(out=rounded_c[:, :, 0:2], in_=y01[:, :, third].rearrange("p t r -> p r t"))
-        codes_a = shared.tile([P, early], U32, name="y_codes_a", offset=held - 512, align_bytes=64)
-        quantize_result(slice(0, 2 * P), codes_a[:, 0 : 2 * P], rounded_a)
-        quantize_result(third, codes_a[:, third], rounded_c)
-        nc.sync.dma_start(out=out_words[:, 0:early], in_=codes_a[:].bitcast(I32))
-        codes_b = keep.tile([P, P], U32, name="y_codes_b", align_bytes=64)
+        rounded_third = shared.tile([P, P, LANES], BF16, name="rounded_third", offset=ROUNDED_THIRD, align_bytes=64)
+        nc.scalar.copy(out=rounded_third[:, :, 2:4], in_=y23[:, :, THIRD].rearrange("p t r -> p r t"))
+        nc.vector.tensor_copy(out=rounded_third[:, :, 0:2], in_=y01[:, :, THIRD].rearrange("p t r -> p r t"))
+        y_codes_early = shared.tile([P, EARLY.stop], U32, name="y_codes_early", offset=EARLY_CODES, align_bytes=64)
+        quantize_result(PAIR, y_codes_early[:, PAIR], rounded_pair)
+        quantize_result(THIRD, y_codes_early[:, THIRD], rounded_third)
+        nc.sync.dma_start(out=out_words[:, EARLY], in_=y_codes_early[:].bitcast(I32))
+        y_codes_last = keep.tile([P, P], U32, name="y_codes_last", align_bytes=64)
 
-        rounded = keep.tile([P, P, LANES], BF16, name="last_rounded", align_bytes=64)
+        rounded_last = keep.tile([P, P, LANES], BF16, name="rounded_last", align_bytes=64)
         y_low = keep.tile([P, 2, P], F32, name="y_low", align_bytes=64)
         y_high = keep.tile([P, 2, P], F32, name="y_high", align_bytes=64)
         nc.vector.tensor_copy(out=y_low[:], in_=low[:])
-        nc.sync.dma_start(out=out_rows[:, 0:2, early:R], in_=y_low[:])
-        nc.vector.tensor_copy(out=rounded[:, :, 0:2], in_=low[:].rearrange("p t r -> p r t"))
-        nc.scalar.copy(out=rounded[:, :, 2:4], in_=high[:].rearrange("p t r -> p r t"))
+        nc.sync.dma_start(out=out_rows[:, 0:2, LAST], in_=y_low[:])
+        nc.vector.tensor_copy(out=rounded_last[:, :, 0:2], in_=low[:].rearrange("p t r -> p r t"))
         nc.scalar.copy(out=y_high[:], in_=high[:])
-        nc.sync.dma_start(out=out_rows[:, 2:4, early:R], in_=y_high[:])
-        quantize_result(slice(early, R), codes_b[:], rounded)
-        nc.sync.dma_start(out=out_words[:, early:R], in_=codes_b[:].bitcast(I32))
+        nc.sync.dma_start(out=out_rows[:, 2:4, LAST], in_=y_high[:])
+        nc.scalar.copy(out=rounded_last[:, :, 2:4], in_=high[:].rearrange("p t r -> p r t"))
+        quantize_result(LAST, y_codes_last[:], rounded_last)
+        nc.sync.dma_start(out=out_words[:, LAST], in_=y_codes_last[:].bitcast(I32))
         for g in range(P // 32):
             queue = nc.scalar if g % 2 == 0 else nc.sync
             queue.dma_start(

@@ -22,16 +22,12 @@ UNITS = 2048
 WINDOW = 4 * UNITS
 PAIR = slice(0, 2 * P)
 THIRD = slice(2 * P, 3 * P)
-EARLY = slice(0, 3 * P)
 LAST = slice(3 * P, R)
-DY2 = 2
-LANE0 = 3
-DY3 = LANE0 + LANES
-LAST_VECTOR_SLOTS = 224
+LANE0 = 0
+DY2 = LANE0 + LANES
+DY3 = DY2 + 1
 AFTER_WINDOWS = (DY3 + 1) * WINDOW
-EARLY_CODES = AFTER_WINDOWS + 1536
-FIRST_HALF = EARLY_CODES + 1536 - 256
-ROUNDED_THIRD = FIRST_HALF + 256
+LATE_VECTOR_SLOTS = 192
 
 FLOPS = 2 * D * R * SLOTS
 
@@ -48,17 +44,16 @@ def tile_attend_gmeprop_x_pl_kernel(tc, dy, wT, offs, out_0, out_1, out_2):
         ring = ctx.enter_context(tc.tile_pool(name="ring", bufs=2))
         shared = ctx.enter_context(tc.tile_pool(name="shared", bufs=1))
         turn = ctx.enter_context(tc.psum_pool(name="turn", bufs=2))
-        sums = ctx.enter_context(tc.psum_pool(name="sums", bufs=2))
-        ends = ctx.enter_context(tc.psum_pool(name="ends", bufs=1))
+        sums = ctx.enter_context(tc.psum_pool(name="sums", bufs=1))
 
         offsets = keep.tile([P, SLOTS // 16], U16, name="offsets")
         dy_pair = keep.tile([P, 2, UNITS], F32, name="dy_pair", align_bytes=64)
         nc.sync.dma_start(out=dy_pair[:], in_=dy[PAIR, :].rearrange("(j p) k -> p j k", j=2))
         nc.sync.dma_start(offsets[:], offs)
-        sources = [dy[THIRD, :]] + [w_rows[:, t, :] for t in range(LANES)] + [dy[LAST, :]]
-        windows = {}
-        for n, source in enumerate(sources, DY2):
-            windows[n] = shared.tile([P, UNITS], F32, name="window%d" % n, offset=n * WINDOW, align_bytes=64)
+        sources = [w_rows[:, t, :] for t in range(LANES)] + [dy[THIRD, :], dy[LAST, :]]
+        windows = []
+        for n, source in enumerate(sources):
+            windows.append(shared.tile([P, UNITS], F32, name="window%d" % n, offset=n * WINDOW, align_bytes=64))
             nc.sync.dma_start(out=windows[n][:], in_=source)
 
         identity = keep.tile([P, P], F32, name="identity")
@@ -97,12 +92,6 @@ def tile_attend_gmeprop_x_pl_kernel(tc, dy, wT, offs, out_0, out_1, out_2):
                 stop=True,
             )
 
-        def multiply_early(t):
-            bank = sums.tile([P, EARLY.stop], F32, name="bank")
-            for cols in (PAIR, THIRD):
-                multiply(bank[:, cols], t, dy_codes[:, cols], dy_scales[:, cols])
-            return bank
-
         def quantize_lane(t, codes, grouped, pieces):
             scales = keep.tile([P, P], U8, name="w_scales%d" % t, align_bytes=64)
             for rows in pieces:
@@ -112,10 +101,17 @@ def tile_attend_gmeprop_x_pl_kernel(tc, dy, wT, offs, out_0, out_1, out_2):
             w_codes.append(codes)
             w_scales.append(scales)
 
+        def quantize_dy(codes, scales, grouped, pieces):
+            for rows in pieces:
+                nc.vector.quantize_mx(
+                    out=codes[:, rows].bitcast(E5M2X4), scales=scales[:, rows], in_=grouped[:, values(rows)]
+                )
+
         def quantize_result(cols, codes, rounded):
             nc.vector.quantize_mx(
-                out=codes.bitcast(E4M3X4), scales=y_scales[:, cols], in_=rounded[:].rearrange("p r t -> p (r t)")
+                out=codes[:].bitcast(E4M3X4), scales=y_scales[:, cols], in_=rounded[:].rearrange("p r t -> p (r t)")
             )
+            nc.sync.dma_start(out=out_words[:, cols], in_=codes[:].bitcast(I32))
 
         w_codes = []
         w_scales = []
@@ -123,7 +119,7 @@ def tile_attend_gmeprop_x_pl_kernel(tc, dy, wT, offs, out_0, out_1, out_2):
         whole = [slice(0, P)]
         halves = [slice(0, P // 2), slice(P // 2, P)]
 
-        dy_grouped = keep.tile([P, LANES * EARLY.stop], BF16, name="dy_grouped", align_bytes=64)
+        dy_grouped = keep.tile([P, LANES * PAIR.stop], BF16, name="dy_grouped", align_bytes=64)
         for j in range(2):
             picked = picked_tile()
             nc.vector.tensor_copy(
@@ -133,25 +129,23 @@ def tile_attend_gmeprop_x_pl_kernel(tc, dy, wT, offs, out_0, out_1, out_2):
             for u in range(2):
                 nc.tensor.transpose(turned[:, u, :], picked[:].bitcast(F32)[:, u * P : (u + 1) * P], identity[:])
             group(turned[:], dy_grouped[:, values(slice(j * P, (j + 1) * P))])
-        group(gather_and_turn(DY2, SLOTS, picked_tile())[:], dy_grouped[:, values(THIRD)])
         w_grouped = [keep.tile([P, LANES * P], BF16, name="w_grouped%d" % t, align_bytes=64) for t in range(2)]
         group(gather_and_turn(LANE0, SLOTS, picked_tile())[:], w_grouped[0][:])
-        dy_codes = shared.tile([P, EARLY.stop], U32, name="dy_codes", offset=LANE0 * WINDOW, align_bytes=64)
-        dy_scales = keep.tile([P, EARLY.stop], U8, name="dy_scales", align_bytes=64)
-        for cols in (PAIR, THIRD):
-            nc.vector.quantize_mx(
-                out=dy_codes[:, cols].bitcast(E5M2X4), scales=dy_scales[:, cols], in_=dy_grouped[:, values(cols)]
-            )
+        dy_codes = shared.tile([P, PAIR.stop], U32, name="dy_codes", offset=LANE0 * WINDOW, align_bytes=64)
+        dy_scales = keep.tile([P, PAIR.stop], U8, name="dy_scales", align_bytes=64)
+        nc.vector.quantize_mx(out=dy_codes[:].bitcast(E5M2X4), scales=dy_scales[:], in_=dy_grouped[:])
 
         picked1 = shared.tile([P, SLOTS], BF16, name="picked1", offset=AFTER_WINDOWS, align_bytes=64)
         group(gather_and_turn(LANE0 + 1, SLOTS, picked1)[:], w_grouped[1][:])
-        y01 = keep.tile([P, 2, EARLY.stop], F32, name="y01", align_bytes=64)
         w_codes0 = shared.tile([P, P], U32, name="w_codes0", offset=AFTER_WINDOWS, align_bytes=64)
+        bank01 = sums.tile([P, 2, PAIR.stop], F32, name="bank01")
         quantize_lane(0, w_codes0, w_grouped[0], whole)
-        nc.scalar.copy(out=y01[:, 0, :], in_=multiply_early(0)[:])
+        multiply(bank01[:, 0, :], 0, dy_codes[:], dy_scales[:])
         quantize_lane(1, keep.tile([P, P], U32, name="w_codes1", align_bytes=64), w_grouped[1], whole)
-        nc.scalar.copy(out=y01[:, 1, :], in_=multiply_early(1)[:])
-        nc.sync.dma_start(out=out_rows[:, 0:2, EARLY], in_=y01[:])
+        multiply(bank01[:, 1, :], 1, dy_codes[:], dy_scales[:])
+        y01 = keep.tile([P, 2, PAIR.stop], F32, name="y01", align_bytes=64)
+        nc.scalar.copy(out=y01[:], in_=bank01[:])
+        nc.sync.dma_start(out=out_rows[:, 0:2, PAIR], in_=y01[:])
 
         turned2 = gather_and_turn(LANE0 + 2, SLOTS, picked_tile())
         turned3 = gather_and_turn(LANE0 + 3, SLOTS // 2, picked_tile())
@@ -161,50 +155,56 @@ def tile_attend_gmeprop_x_pl_kernel(tc, dy, wT, offs, out_0, out_1, out_2):
         rounded_pair = shared.tile(
             [P, PAIR.stop, LANES], BF16, name="rounded_pair", offset=lane3_bytes + WINDOW // 2, align_bytes=64
         )
-        nc.vector.tensor_copy(out=rounded_pair[:, :, 0:2], in_=y01[:, :, PAIR].rearrange("p t r -> p r t"))
+        nc.vector.tensor_copy(out=rounded_pair[:, :, 0:2], in_=y01[:].rearrange("p t r -> p r t"))
         quantize_lane(2, keep.tile([P, P], U32, name="w_codes2", align_bytes=64), w_grouped2, whole)
-        pair_bank = ends.tile([P, 2, PAIR.stop], F32, name="pair_bank")
-        third_bank = ends.tile([P, 2, P], F32, name="third_bank")
-        multiply(pair_bank[:, 0, :], 2, dy_codes[:, PAIR], dy_scales[:, PAIR])
-        multiply(third_bank[:, 0, :], 2, dy_codes[:, THIRD], dy_scales[:, THIRD])
+        bank23 = sums.tile([P, 2, PAIR.stop], F32, name="bank23")
+        multiply(bank23[:, 0, :], 2, dy_codes[:], dy_scales[:])
         w_grouped3 = keep.tile([P, LANES * P], BF16, name="w_grouped3", align_bytes=64)
         for rows in halves:
             group(turned3[:, :, rows], w_grouped3[:, values(rows)])
         quantize_lane(3, keep.tile([P, P], U32, name="w_codes3", align_bytes=64), w_grouped3, halves)
-        multiply(pair_bank[:, 1, :], 3, dy_codes[:, PAIR], dy_scales[:, PAIR])
-        multiply(third_bank[:, 1, :], 3, dy_codes[:, THIRD], dy_scales[:, THIRD])
+        multiply(bank23[:, 1, :], 3, dy_codes[:], dy_scales[:])
 
-        turned = gather_and_turn(DY3, LAST_VECTOR_SLOTS, picked_tile())
-        y23 = shared.tile([P, 2, EARLY.stop], F32, name="y23", offset=DY3 * WINDOW, align_bytes=64)
+        turned = gather_and_turn(DY2, LATE_VECTOR_SLOTS, picked_tile())
+        y23 = shared.tile([P, 2, PAIR.stop], F32, name="y23", offset=DY2 * WINDOW, align_bytes=64)
         pair_tiles = [slice(j * P, (j + 1) * P) for j in range(2)]
         for cols in pair_tiles:
-            nc.scalar.copy(out=y23[:, :, cols], in_=pair_bank[:, :, cols])
-        nc.vector.tensor_copy(out=y23[:, :, THIRD], in_=third_bank[:])
-        nc.sync.dma_start(out=out_rows[:, 2:4, EARLY], in_=y23[:])
+            nc.scalar.copy(out=y23[:, :, cols], in_=bank23[:, :, cols])
+        nc.sync.dma_start(out=out_rows[:, 2:4, PAIR], in_=y23[:])
         for cols in pair_tiles:
             nc.vector.tensor_copy(out=rounded_pair[:, cols, 2:4], in_=y23[:, :, cols].rearrange("p t r -> p r t"))
+        third_grouped = keep.tile([P, LANES * P], BF16, name="third_grouped", align_bytes=64)
+        group(turned[:], third_grouped[:])
 
-        first_half = shared.tile([P, LANES * P // 2], BF16, name="first_half", offset=FIRST_HALF, align_bytes=64)
-        second_half = keep.tile([P, LANES * P // 2], BF16, name="second_half", align_bytes=64)
+        turned = gather_and_turn(DY3, SLOTS // 2, picked_tile())
+        third_codes = shared.tile([P, P], U32, name="third_codes", offset=DY3 * WINDOW, align_bytes=64)
+        third_scales = keep.tile([P, P], U8, name="third_scales", align_bytes=64)
+        quantize_dy(third_codes, third_scales, third_grouped, whole)
+        pair_codes = shared.tile(
+            [P, PAIR.stop], U32, name="pair_codes", offset=DY3 * WINDOW + WINDOW // 2, align_bytes=64
+        )
+        quantize_result(PAIR, pair_codes, rounded_pair)
+        third_low = sums.tile([P, 2, P], F32, name="third_low")
+        third_high = sums.tile([P, 2, P], F32, name="third_high")
+        for t in range(LANES):
+            multiply((third_low, third_high)[t // 2][:, t % 2, :], t, third_codes[:], third_scales[:])
+        last_grouped = keep.tile([P, LANES * P], BF16, name="last_grouped", align_bytes=64)
         last_codes = keep.tile([P, P], U32, name="last_codes", align_bytes=64)
         last_scales = keep.tile([P, P], U8, name="last_scales", align_bytes=64)
-        for rows, grouped in zip(halves, (first_half, second_half)):
-            group(turned[:, :, rows], grouped[:])
-        for rows, grouped in zip(halves, (first_half, second_half)):
-            nc.vector.quantize_mx(out=last_codes[:, rows].bitcast(E5M2X4), scales=last_scales[:, rows], in_=grouped[:])
-        low = ends.tile([P, 2, P], F32, name="low")
-        high = ends.tile([P, 2, P], F32, name="high")
+        for rows in halves:
+            group(turned[:, :, rows], last_grouped[:, values(rows)])
+        quantize_dy(last_codes, last_scales, last_grouped, halves)
+        low = sums.tile([P, 2, P], F32, name="low")
+        high = sums.tile([P, 2, P], F32, name="high")
         for t in range(LANES):
             multiply((low, high)[t // 2][:, t % 2, :], t, last_codes[:], last_scales[:])
-
-        rounded_third = shared.tile([P, P, LANES], BF16, name="rounded_third", offset=ROUNDED_THIRD, align_bytes=64)
-        nc.scalar.copy(out=rounded_third[:, :, 2:4], in_=y23[:, :, THIRD].rearrange("p t r -> p r t"))
-        nc.vector.tensor_copy(out=rounded_third[:, :, 0:2], in_=y01[:, :, THIRD].rearrange("p t r -> p r t"))
-        y_codes_early = shared.tile([P, EARLY.stop], U32, name="y_codes_early", offset=EARLY_CODES, align_bytes=64)
-        quantize_result(PAIR, y_codes_early[:, PAIR], rounded_pair)
-        quantize_result(THIRD, y_codes_early[:, THIRD], rounded_third)
-        nc.sync.dma_start(out=out_words[:, EARLY], in_=y_codes_early[:].bitcast(I32))
-        y_codes_last = keep.tile([P, P], U32, name="y_codes_last", align_bytes=64)
+        y_third = keep.tile([P, LANES, P], F32, name="y_third", align_bytes=64)
+        rounded_third = keep.tile([P, P, LANES], BF16, name="rounded_third", align_bytes=64)
+        nc.scalar.copy(out=y_third[:, 0:2, :], in_=third_low[:])
+        nc.vector.tensor_copy(out=y_third[:, 2:4, :], in_=third_high[:])
+        nc.sync.dma_start(out=out_rows[:, :, THIRD], in_=y_third[:])
+        nc.scalar.copy(out=rounded_third[:, :, 0:2], in_=third_low[:].rearrange("p t r -> p r t"))
+        nc.scalar.copy(out=rounded_third[:, :, 2:4], in_=third_high[:].rearrange("p t r -> p r t"))
 
         rounded_last = keep.tile([P, P, LANES], BF16, name="rounded_last", align_bytes=64)
         y_low = keep.tile([P, 2, P], F32, name="y_low", align_bytes=64)
@@ -212,11 +212,11 @@ def tile_attend_gmeprop_x_pl_kernel(tc, dy, wT, offs, out_0, out_1, out_2):
         nc.vector.tensor_copy(out=y_low[:], in_=low[:])
         nc.sync.dma_start(out=out_rows[:, 0:2, LAST], in_=y_low[:])
         nc.vector.tensor_copy(out=rounded_last[:, :, 0:2], in_=low[:].rearrange("p t r -> p r t"))
+        quantize_result(THIRD, keep.tile([P, P], U32, name="y_codes_third", align_bytes=64), rounded_third)
         nc.scalar.copy(out=y_high[:], in_=high[:])
         nc.sync.dma_start(out=out_rows[:, 2:4, LAST], in_=y_high[:])
         nc.scalar.copy(out=rounded_last[:, :, 2:4], in_=high[:].rearrange("p t r -> p r t"))
-        quantize_result(LAST, y_codes_last[:], rounded_last)
-        nc.sync.dma_start(out=out_words[:, LAST], in_=y_codes_last[:].bitcast(I32))
+        quantize_result(LAST, keep.tile([P, P], U32, name="y_codes_last", align_bytes=64), rounded_last)
         for g in range(P // 32):
             queue = nc.scalar if g % 2 == 0 else nc.sync
             queue.dma_start(

@@ -109,9 +109,8 @@ def tile_attend_gmeprop_x_pl_kernel(tc, dy, wT, offs, out_0, out_1, out_2):
 
         def quantize_result(cols, codes, rounded):
             nc.vector.quantize_mx(
-                out=codes[:].bitcast(E4M3X4), scales=y_scales[:, cols], in_=rounded[:].rearrange("p r t -> p (r t)")
+                out=codes.bitcast(E4M3X4), scales=y_scales[:, cols], in_=rounded[:].rearrange("p r t -> p (r t)")
             )
-            nc.sync.dma_start(out=out_words[:, cols], in_=codes[:].bitcast(I32))
 
         w_codes = []
         w_scales = []
@@ -183,7 +182,8 @@ def tile_attend_gmeprop_x_pl_kernel(tc, dy, wT, offs, out_0, out_1, out_2):
         pair_codes = shared.tile(
             [P, PAIR.stop], U32, name="pair_codes", offset=DY3 * WINDOW + WINDOW // 2, align_bytes=64
         )
-        quantize_result(PAIR, pair_codes, rounded_pair)
+        quantize_result(PAIR, pair_codes[:], rounded_pair)
+        nc.sync.dma_start(out=out_words[:, PAIR], in_=pair_codes[:].bitcast(I32))
         third_low = sums.tile([P, 2, P], F32, name="third_low")
         third_high = sums.tile([P, 2, P], F32, name="third_high")
         for t in range(LANES):
@@ -201,8 +201,9 @@ def tile_attend_gmeprop_x_pl_kernel(tc, dy, wT, offs, out_0, out_1, out_2):
         y_third = keep.tile([P, LANES, P], F32, name="y_third", align_bytes=64)
         rounded_third = keep.tile([P, P, LANES], BF16, name="rounded_third", align_bytes=64)
         nc.scalar.copy(out=y_third[:, 0:2, :], in_=third_low[:])
+        nc.sync.dma_start(out=out_rows[:, 0:2, THIRD], in_=y_third[:, 0:2, :])
         nc.vector.tensor_copy(out=y_third[:, 2:4, :], in_=third_high[:])
-        nc.sync.dma_start(out=out_rows[:, :, THIRD], in_=y_third[:])
+        nc.sync.dma_start(out=out_rows[:, 2:4, THIRD], in_=y_third[:, 2:4, :])
         nc.scalar.copy(out=rounded_third[:, :, 0:2], in_=third_low[:].rearrange("p t r -> p r t"))
         nc.scalar.copy(out=rounded_third[:, :, 2:4], in_=third_high[:].rearrange("p t r -> p r t"))
 
@@ -212,11 +213,13 @@ def tile_attend_gmeprop_x_pl_kernel(tc, dy, wT, offs, out_0, out_1, out_2):
         nc.vector.tensor_copy(out=y_low[:], in_=low[:])
         nc.sync.dma_start(out=out_rows[:, 0:2, LAST], in_=y_low[:])
         nc.vector.tensor_copy(out=rounded_last[:, :, 0:2], in_=low[:].rearrange("p t r -> p r t"))
-        quantize_result(THIRD, keep.tile([P, P], U32, name="y_codes_third", align_bytes=64), rounded_third)
+        late_codes = keep.tile([P, 2 * P], U32, name="late_codes", align_bytes=64)
+        quantize_result(THIRD, late_codes[:, 0:P], rounded_third)
         nc.scalar.copy(out=y_high[:], in_=high[:])
         nc.sync.dma_start(out=out_rows[:, 2:4, LAST], in_=y_high[:])
         nc.scalar.copy(out=rounded_last[:, :, 2:4], in_=high[:].rearrange("p t r -> p r t"))
-        quantize_result(LAST, keep.tile([P, P], U32, name="y_codes_last", align_bytes=64), rounded_last)
+        quantize_result(LAST, late_codes[:, P : 2 * P], rounded_last)
+        nc.sync.dma_start(out=out_words[:, PAIR.stop : R], in_=late_codes[:].bitcast(I32))
         for g in range(P // 32):
             queue = nc.scalar if g % 2 == 0 else nc.sync
             queue.dma_start(

@@ -107,9 +107,14 @@ def tile_attend_gmeprop_x_pl_kernel(tc, dy, wT, offs, out_0, out_1, out_2):
                     out=codes[:, rows].bitcast(E5M2X4), scales=scales[:, rows], in_=grouped[:, values(rows)]
                 )
 
+        def round_result(rounded, y):
+            nc.vector.tensor_copy(
+                out=rounded.rearrange("p (c i) t -> p c t i", i=4), in_=y.rearrange("p t (c i) -> p c t i", i=4)
+            )
+
         def quantize_result(cols, codes, rounded):
             nc.vector.quantize_mx(
-                out=codes.bitcast(E4M3X4), scales=y_scales[:, cols], in_=rounded[:].rearrange("p r t -> p (r t)")
+                out=codes.bitcast(E4M3X4), scales=y_scales[:, cols], in_=rounded.rearrange("p r t -> p (r t)")
             )
 
         w_codes = []
@@ -182,7 +187,7 @@ def tile_attend_gmeprop_x_pl_kernel(tc, dy, wT, offs, out_0, out_1, out_2):
         pair_codes = shared.tile(
             [P, PAIR.stop], U32, name="pair_codes", offset=DY3 * WINDOW + WINDOW // 2, align_bytes=64
         )
-        quantize_result(PAIR, pair_codes[:], rounded_pair)
+        quantize_result(PAIR, pair_codes[:], rounded_pair[:])
         nc.sync.dma_start(out=out_words[:, PAIR], in_=pair_codes[:].bitcast(I32))
         third_low = sums.tile([P, 2, P], F32, name="third_low")
         third_high = sums.tile([P, 2, P], F32, name="third_high")
@@ -194,31 +199,35 @@ def tile_attend_gmeprop_x_pl_kernel(tc, dy, wT, offs, out_0, out_1, out_2):
         for rows in halves:
             group(turned[:, :, rows], last_grouped[:, values(rows)])
         quantize_dy(last_codes, last_scales, last_grouped, halves)
-        low = sums.tile([P, 2, P], F32, name="low")
-        high = sums.tile([P, 2, P], F32, name="high")
+        last_banks = [sums.tile([P, P], F32, name=name) for name in ("low", "high", "bank01", "bank23")]
         for t in range(LANES):
-            multiply((low, high)[t // 2][:, t % 2, :], t, last_codes[:], last_scales[:])
+            multiply(last_banks[t][:], t, last_codes[:], last_scales[:])
         y_third = keep.tile([P, LANES, P], F32, name="y_third", align_bytes=64)
+        for lanes, bank in zip((slice(0, 2), slice(2, 4)), (third_low, third_high)):
+            nc.scalar.copy(out=y_third[:, lanes, :], in_=bank[:])
+            nc.sync.dma_start(out=out_rows[:, lanes, THIRD], in_=y_third[:, lanes, :])
         rounded_third = keep.tile([P, P, LANES], BF16, name="rounded_third", align_bytes=64)
-        nc.scalar.copy(out=y_third[:, 0:2, :], in_=third_low[:])
-        nc.sync.dma_start(out=out_rows[:, 0:2, THIRD], in_=y_third[:, 0:2, :])
-        nc.vector.tensor_copy(out=y_third[:, 2:4, :], in_=third_high[:])
-        nc.sync.dma_start(out=out_rows[:, 2:4, THIRD], in_=y_third[:, 2:4, :])
-        nc.scalar.copy(out=rounded_third[:, :, 0:2], in_=third_low[:].rearrange("p t r -> p r t"))
-        nc.scalar.copy(out=rounded_third[:, :, 2:4], in_=third_high[:].rearrange("p t r -> p r t"))
+        round_result(rounded_third[:], y_third[:])
 
         rounded_last = keep.tile([P, P, LANES], BF16, name="rounded_last", align_bytes=64)
-        y_low = keep.tile([P, 2, P], F32, name="y_low", align_bytes=64)
-        y_high = keep.tile([P, 2, P], F32, name="y_high", align_bytes=64)
-        nc.vector.tensor_copy(out=y_low[:], in_=low[:])
-        nc.sync.dma_start(out=out_rows[:, 0:2, LAST], in_=y_low[:])
-        nc.vector.tensor_copy(out=rounded_last[:, :, 0:2], in_=low[:].rearrange("p t r -> p r t"))
+        y_last = keep.tile([P, LANES, P], F32, name="y_last", align_bytes=64)
         late_codes = keep.tile([P, 2 * P], U32, name="late_codes", align_bytes=64)
-        quantize_result(THIRD, late_codes[:, 0:P], rounded_third)
-        nc.scalar.copy(out=y_high[:], in_=high[:])
-        nc.sync.dma_start(out=out_rows[:, 2:4, LAST], in_=y_high[:])
-        nc.scalar.copy(out=rounded_last[:, :, 2:4], in_=high[:].rearrange("p t r -> p r t"))
-        quantize_result(LAST, late_codes[:, P : 2 * P], rounded_last)
+        for t in range(2):
+            nc.scalar.copy(out=y_last[:, t, :], in_=last_banks[t][:])
+        nc.sync.dma_start(out=out_rows[:, 0:2, LAST], in_=y_last[:, 0:2, :])
+        quantize_result(THIRD, late_codes[:, 0:P], rounded_third[:])
+        nc.scalar.copy(out=y_last[:, 2, :], in_=last_banks[2][:])
+        for cols in halves:
+            nc.scalar.copy(out=y_last[:, 3, cols], in_=last_banks[3][:, cols])
+        nc.sync.dma_start(out=out_rows[:, 2:4, LAST], in_=y_last[:, 2:4, :])
+        for cols in halves:
+            round_result(rounded_last[:, cols, :], y_last[:, :, cols])
+        for cols in halves:
+            quantize_result(
+                slice(LAST.start + cols.start, LAST.start + cols.stop),
+                late_codes[:, P + cols.start : P + cols.stop],
+                rounded_last[:, cols, :],
+            )
         nc.sync.dma_start(out=out_words[:, PAIR.stop : R], in_=late_codes[:].bitcast(I32))
         for g in range(P // 32):
             queue = nc.scalar if g % 2 == 0 else nc.sync

@@ -48,7 +48,7 @@ def tile_attend_gmeprop_x_pl_kernel(tc, dy, wT, offs, out_0, out_1, out_2):
 
         offsets = keep.tile([P, SLOTS // 16], U16, name="offsets")
         dy_pair = keep.tile([P, 2, UNITS], F32, name="dy_pair", align_bytes=64)
-        nc.sync.dma_start(out=dy_pair[:], in_=dy[PAIR, :].rearrange("(j p) k -> p j k", j=2))
+        nc.sync.dma_start(out=dy_pair[:], in_=dy[PAIR, :].rearrange("(p j) k -> p j k", j=2))
         nc.sync.dma_start(offsets[:], offs)
         sources = [w_rows[:, t, :] for t in range(LANES)] + [dy[THIRD, :], dy[LAST, :]]
         windows = []
@@ -124,15 +124,18 @@ def tile_attend_gmeprop_x_pl_kernel(tc, dy, wT, offs, out_0, out_1, out_2):
         halves = [slice(0, P // 2), slice(P // 2, P)]
 
         dy_grouped = keep.tile([P, LANES * PAIR.stop], BF16, name="dy_grouped", align_bytes=64)
+        turned = turn.tile([P, 2, 2, P], F32, name="turned")
         for j in range(2):
             picked = picked_tile()
             nc.vector.tensor_copy(
                 picked[:].rearrange("p (u s c) -> p s u c", u=2, c=2), dy_pair[:, j, :].indirect(offsets[:])
             )
-            turned = turn.tile([P, 2, P], F32, name="turned")
             for u in range(2):
-                nc.tensor.transpose(turned[:, u, :], picked[:].bitcast(F32)[:, u * P : (u + 1) * P], identity[:])
-            group(turned[:], dy_grouped[:, values(slice(j * P, (j + 1) * P))])
+                nc.tensor.transpose(turned[:, j, u, :], picked[:].bitcast(F32)[:, u * P : (u + 1) * P], identity[:])
+        nc.scalar.copy(
+            out=dy_grouped[:].bitcast(F32).rearrange("p (m j u) -> p m j u", j=2, u=2),
+            in_=turned[:].rearrange("p j u m -> p m j u"),
+        )
         w_grouped = [keep.tile([P, LANES * P], BF16, name="w_grouped%d" % t, align_bytes=64) for t in range(2)]
         group(gather_and_turn(LANE0, SLOTS, picked_tile())[:], w_grouped[0][:])
         dy_codes = shared.tile([P, PAIR.stop], U32, name="dy_codes", offset=LANE0 * WINDOW, align_bytes=64)
@@ -147,19 +150,15 @@ def tile_attend_gmeprop_x_pl_kernel(tc, dy, wT, offs, out_0, out_1, out_2):
         multiply(bank01[:, 0, :], 0, dy_codes[:], dy_scales[:])
         quantize_lane(1, keep.tile([P, P], U32, name="w_codes1", align_bytes=64), w_grouped[1], whole)
         multiply(bank01[:, 1, :], 1, dy_codes[:], dy_scales[:])
-        y01 = keep.tile([P, 2, PAIR.stop], F32, name="y01", align_bytes=64)
-        nc.scalar.copy(out=y01[:], in_=bank01[:])
-        nc.sync.dma_start(out=out_rows[:, 0:2, PAIR], in_=y01[:])
 
         turned2 = gather_and_turn(LANE0 + 2, SLOTS, picked_tile())
         turned3 = gather_and_turn(LANE0 + 3, SLOTS // 2, picked_tile())
         lane3_bytes = (LANE0 + 3) * WINDOW
         w_grouped2 = shared.tile([P, LANES * P], BF16, name="w_grouped2", offset=lane3_bytes, align_bytes=64)
         group(turned2[:], w_grouped2[:])
-        rounded_pair = shared.tile(
-            [P, PAIR.stop, LANES], BF16, name="rounded_pair", offset=lane3_bytes + WINDOW // 2, align_bytes=64
-        )
-        nc.vector.tensor_copy(out=rounded_pair[:, :, 0:2], in_=y01[:].rearrange("p t r -> p r t"))
+        y01 = shared.tile([P, 2, PAIR.stop], F32, name="y01", offset=lane3_bytes + WINDOW // 2, align_bytes=64)
+        nc.vector.tensor_copy(out=y01[:], in_=bank01[:])
+        nc.sync.dma_start(out=out_rows[:, 0:2, PAIR], in_=y01[:])
         quantize_lane(2, keep.tile([P, P], U32, name="w_codes2", align_bytes=64), w_grouped2, whole)
         bank23 = sums.tile([P, 2, PAIR.stop], F32, name="bank23")
         multiply(bank23[:, 0, :], 2, dy_codes[:], dy_scales[:])
@@ -171,6 +170,10 @@ def tile_attend_gmeprop_x_pl_kernel(tc, dy, wT, offs, out_0, out_1, out_2):
 
         turned = gather_and_turn(DY2, LATE_VECTOR_SLOTS, picked_tile())
         y23 = shared.tile([P, 2, PAIR.stop], F32, name="y23", offset=DY2 * WINDOW, align_bytes=64)
+        rounded_pair = shared.tile(
+            [P, PAIR.stop, LANES], BF16, name="rounded_pair", offset=DY2 * WINDOW + WINDOW // 2, align_bytes=64
+        )
+        nc.vector.tensor_copy(out=rounded_pair[:, :, 0:2], in_=y01[:].rearrange("p t r -> p r t"))
         pair_tiles = [slice(j * P, (j + 1) * P) for j in range(2)]
         for cols in pair_tiles:
             nc.scalar.copy(out=y23[:, :, cols], in_=bank23[:, :, cols])
@@ -180,7 +183,7 @@ def tile_attend_gmeprop_x_pl_kernel(tc, dy, wT, offs, out_0, out_1, out_2):
         third_grouped = keep.tile([P, LANES * P], BF16, name="third_grouped", align_bytes=64)
         group(turned[:], third_grouped[:])
 
-        turned = gather_and_turn(DY3, SLOTS // 2, picked_tile())
+        turned = gather_and_turn(DY3, 288, picked_tile())
         third_codes = shared.tile([P, P], U32, name="third_codes", offset=DY3 * WINDOW, align_bytes=64)
         third_scales = keep.tile([P, P], U8, name="third_scales", align_bytes=64)
         quantize_dy(third_codes, third_scales, third_grouped, whole)

@@ -183,7 +183,7 @@ def tile_attend_gmeprop_x_pl_kernel(tc, dy, wT, offs, out_0, out_1, out_2):
         third_grouped = keep.tile([P, LANES * P], BF16, name="third_grouped", align_bytes=64)
         group(turned[:], third_grouped[:])
 
-        turned = gather_and_turn(DY3, 288, picked_tile())
+        turned = gather_and_turn(DY3, SLOTS // 2, picked_tile())
         third_codes = shared.tile([P, P], U32, name="third_codes", offset=DY3 * WINDOW, align_bytes=64)
         third_scales = keep.tile([P, P], U8, name="third_scales", align_bytes=64)
         quantize_dy(third_codes, third_scales, third_grouped, whole)

@@ -23,11 +23,10 @@ WINDOW = 4 * UNITS
 PAIR = slice(0, 2 * P)
 THIRD = slice(2 * P, 3 * P)
 LAST = slice(3 * P, R)
-LANE0 = 0
-DY2 = LANE0 + LANES
-DY3 = DY2 + 1
-AFTER_WINDOWS = (DY3 + 1) * WINDOW
-LATE_VECTOR_SLOTS = 192
+DY2 = 0
+DY3 = 1
+LANES23 = 2
+AFTER_WINDOWS = 4 * WINDOW
 
 FLOPS = 2 * D * R * SLOTS
 
@@ -41,7 +40,7 @@ def tile_attend_gmeprop_x_pl_kernel(tc, dy, wT, offs, out_0, out_1, out_2):
 
     with ExitStack() as ctx:
         keep = ctx.enter_context(tc.tile_pool(name="keep", bufs=1))
-        ring = ctx.enter_context(tc.tile_pool(name="ring", bufs=2))
+        ring = ctx.enter_context(tc.tile_pool(name="ring", bufs=3))
         shared = ctx.enter_context(tc.tile_pool(name="shared", bufs=1))
         turn = ctx.enter_context(tc.psum_pool(name="turn", bufs=2))
         sums = ctx.enter_context(tc.psum_pool(name="sums", bufs=1))
@@ -50,31 +49,47 @@ def tile_attend_gmeprop_x_pl_kernel(tc, dy, wT, offs, out_0, out_1, out_2):
         dy_pair = keep.tile([P, 2, UNITS], F32, name="dy_pair", align_bytes=64)
         nc.sync.dma_start(out=dy_pair[:], in_=dy[PAIR, :].rearrange("(p j) k -> p j k", j=2))
         nc.sync.dma_start(offsets[:], offs)
-        sources = [w_rows[:, t, :] for t in range(LANES)] + [dy[THIRD, :], dy[LAST, :]]
+        w_pairs = [
+            keep.tile([P, 2 * UNITS], F32, name="w_pair0", align_bytes=64),
+            shared.tile([P, 2 * UNITS], F32, name="w_pair1", offset=LANES23 * WINDOW, align_bytes=64),
+        ]
+        for h in range(2):
+            nc.sync.dma_start(
+                out=w_pairs[h][:].rearrange("p (j k) -> p j k", j=2), in_=w_rows[:, 2 * h : 2 * h + 2, :]
+            )
         windows = []
-        for n, source in enumerate(sources):
+        for n, rows in enumerate((THIRD, LAST)):
             windows.append(shared.tile([P, UNITS], F32, name="window%d" % n, offset=n * WINDOW, align_bytes=64))
-            nc.sync.dma_start(out=windows[n][:], in_=source)
+            nc.sync.dma_start(out=windows[n][:], in_=dy[rows, :])
 
         identity = keep.tile([P, P], F32, name="identity")
         make_identity(nc, identity[:])
 
-        def gather_and_turn(n, vector_slots, picked):
-            split = vector_slots // 16
-            nc.vector.tensor_copy(picked[:, 0:vector_slots], windows[n][:].indirect(offsets[:, 0:split]))
-            if vector_slots < SLOTS:
-                nc.scalar.activation(picked[:, vector_slots:SLOTS], windows[n][:].indirect(offsets[:, split:]), COPY)
-            words = picked[:].bitcast(F32)
-            turned = turn.tile([P, 2, P], F32, name="turned")
-            for u in range(2):
-                nc.tensor.transpose(turned[:, u, :], words[:, u : 2 * P : 2], identity[:])
-            return turned
-
         def picked_tile():
             return ring.tile([P, SLOTS], BF16, name="picked", align_bytes=64)
 
-        def group(turned, grouped):
-            nc.scalar.copy(
+        def turn_as_listed(picked, turned):
+            words = picked[:].bitcast(F32)
+            for u in range(2):
+                nc.tensor.transpose(turned[:, u, :], words[:, u : 2 * P : 2], identity[:])
+
+        def gather_dealt_and_turn(window, turned):
+            picked = picked_tile()
+            nc.vector.tensor_copy(
+                picked[:].rearrange("p (u s c) -> p s u c", u=2, c=2), window.indirect(offsets[:])
+            )
+            for u in range(2):
+                nc.tensor.transpose(turned[:, u, :], picked[:].bitcast(F32)[:, u * P : (u + 1) * P], identity[:])
+
+        def gather_shared_and_turn(window, turned):
+            picked = picked_tile()
+            half = SLOTS // 2
+            nc.vector.tensor_copy(picked[:, 0:half], window.indirect(offsets[:, 0 : half // 16]))
+            nc.scalar.activation(picked[:, half:SLOTS], window.indirect(offsets[:, half // 16 :]), COPY)
+            turn_as_listed(picked, turned)
+
+        def grouping(turned, grouped):
+            return dict(
                 out=grouped.bitcast(F32).rearrange("p (m u) -> p m u", u=2), in_=turned.rearrange("p u m -> p m u")
             )
 
@@ -82,22 +97,34 @@ def tile_attend_gmeprop_x_pl_kernel(tc, dy, wT, offs, out_0, out_1, out_2):
             return slice(LANES * cols.start, LANES * cols.stop)
 
         def multiply(out, t, codes, scales):
+            lane = slice(t % 2 * P, (t % 2 + 1) * P)
             nc.tensor.matmul_mx(
                 out=out,
-                lhsT=w_codes[t][:].bitcast(E4M3X4),
-                lhsT_scale=w_scales[t][:],
+                lhsT=w_codes[t // 2][:, lane].bitcast(E4M3X4),
+                lhsT_scale=w_scales[t // 2][:, lane],
                 rhs=codes.bitcast(E5M2X4),
                 rhs_scale=scales,
                 start=True,
                 stop=True,
             )
 
-        def quantize_lane(t, codes, grouped, pieces):
-            scales = keep.tile([P, P], U8, name="w_scales%d" % t, align_bytes=64)
-            for rows in pieces:
-                nc.vector.quantize_mx(
-                    out=codes[:, rows].bitcast(E4M3X4), scales=scales[:, rows], in_=grouped[:, values(rows)]
-                )
+        def gather_lanes(h):
+            turned_odd = turn.tile([P, 2, P], F32, name="turned")
+            gather_dealt_and_turn(w_pairs[h][:, UNITS : 2 * UNITS], turned_odd)
+            picked = picked_tile()
+            nc.scalar.activation(picked[:], w_pairs[h][:].indirect(offsets[:]), COPY)
+            turned_even = turn.tile([P, 2, P], F32, name="turned")
+            turn_as_listed(picked, turned_even)
+            return turned_even, turned_odd
+
+        def group_lanes(turned_even, turned_odd, grouped):
+            nc.vector.tensor_copy(**grouping(turned_odd[:], grouped[:, 1, :]))
+            nc.scalar.copy(**grouping(turned_even[:], grouped[:, 0, :]))
+
+        def quantize_lanes(h, codes, grouped):
+            scales = keep.tile([P, 2 * P], U8, name="w_scales%d" % h, align_bytes=64)
+            for j, cols in enumerate(pair_tiles):
+                nc.vector.quantize_mx(out=codes[:, cols].bitcast(E4M3X4), scales=scales[:, cols], in_=grouped[:, j, :])
             w_codes.append(codes)
             w_scales.append(scales)
 
@@ -122,89 +149,73 @@ def tile_attend_gmeprop_x_pl_kernel(tc, dy, wT, offs, out_0, out_1, out_2):
         y_scales = keep.tile([P, R], U8, name="y_scales", align_bytes=64)
         whole = [slice(0, P)]
         halves = [slice(0, P // 2), slice(P // 2, P)]
+        pair_tiles = [slice(j * P, (j + 1) * P) for j in range(2)]
 
         dy_grouped = keep.tile([P, LANES * PAIR.stop], BF16, name="dy_grouped", align_bytes=64)
         turned = turn.tile([P, 2, 2, P], F32, name="turned")
         for j in range(2):
-            picked = picked_tile()
-            nc.vector.tensor_copy(
-                picked[:].rearrange("p (u s c) -> p s u c", u=2, c=2), dy_pair[:, j, :].indirect(offsets[:])
-            )
-            for u in range(2):
-                nc.tensor.transpose(turned[:, j, u, :], picked[:].bitcast(F32)[:, u * P : (u + 1) * P], identity[:])
+            gather_dealt_and_turn(dy_pair[:, j, :], turned[:, j])
         nc.scalar.copy(
             out=dy_grouped[:].bitcast(F32).rearrange("p (m j u) -> p m j u", j=2, u=2),
             in_=turned[:].rearrange("p j u m -> p m j u"),
         )
-        w_grouped = [keep.tile([P, LANES * P], BF16, name="w_grouped%d" % t, align_bytes=64) for t in range(2)]
-        group(gather_and_turn(LANE0, SLOTS, picked_tile())[:], w_grouped[0][:])
-        dy_codes = shared.tile([P, PAIR.stop], U32, name="dy_codes", offset=LANE0 * WINDOW, align_bytes=64)
+        dy_codes = keep.tile([P, PAIR.stop], U32, name="dy_codes", align_bytes=64)
         dy_scales = keep.tile([P, PAIR.stop], U8, name="dy_scales", align_bytes=64)
         nc.vector.quantize_mx(out=dy_codes[:].bitcast(E5M2X4), scales=dy_scales[:], in_=dy_grouped[:])
 
-        picked1 = shared.tile([P, SLOTS], BF16, name="picked1", offset=AFTER_WINDOWS, align_bytes=64)
-        group(gather_and_turn(LANE0 + 1, SLOTS, picked1)[:], w_grouped[1][:])
-        w_codes0 = shared.tile([P, P], U32, name="w_codes0", offset=AFTER_WINDOWS, align_bytes=64)
+        grouped = keep.tile([P, 2, LANES * P], BF16, name="w_grouped0", align_bytes=64)
+        group_lanes(*gather_lanes(0), grouped)
+        quantize_lanes(0, keep.tile([P, 2 * P], U32, name="w_codes0", align_bytes=64), grouped)
         bank01 = sums.tile([P, 2, PAIR.stop], F32, name="bank01")
-        quantize_lane(0, w_codes0, w_grouped[0], whole)
-        multiply(bank01[:, 0, :], 0, dy_codes[:], dy_scales[:])
-        quantize_lane(1, keep.tile([P, P], U32, name="w_codes1", align_bytes=64), w_grouped[1], whole)
-        multiply(bank01[:, 1, :], 1, dy_codes[:], dy_scales[:])
+        for t in range(2):
+            multiply(bank01[:, t, :], t, dy_codes[:], dy_scales[:])
 
-        turned2 = gather_and_turn(LANE0 + 2, SLOTS, picked_tile())
-        turned3 = gather_and_turn(LANE0 + 3, SLOTS // 2, picked_tile())
-        lane3_bytes = (LANE0 + 3) * WINDOW
-        w_grouped2 = shared.tile([P, LANES * P], BF16, name="w_grouped2", offset=lane3_bytes, align_bytes=64)
-        group(turned2[:], w_grouped2[:])
-        y01 = shared.tile([P, 2, PAIR.stop], F32, name="y01", offset=lane3_bytes + WINDOW // 2, align_bytes=64)
-        nc.vector.tensor_copy(out=y01[:], in_=bank01[:])
+        turned_lanes = gather_lanes(1)
+        y01 = shared.tile([P, 2, PAIR.stop], F32, name="y01", offset=LANES23 * WINDOW, align_bytes=64)
+        nc.scalar.copy(out=y01[:], in_=bank01[:])
         nc.sync.dma_start(out=out_rows[:, 0:2, PAIR], in_=y01[:])
-        quantize_lane(2, keep.tile([P, P], U32, name="w_codes2", align_bytes=64), w_grouped2, whole)
-        bank23 = sums.tile([P, 2, PAIR.stop], F32, name="bank23")
-        multiply(bank23[:, 0, :], 2, dy_codes[:], dy_scales[:])
-        w_grouped3 = keep.tile([P, LANES * P], BF16, name="w_grouped3", align_bytes=64)
-        for rows in halves:
-            group(turned3[:, :, rows], w_grouped3[:, values(rows)])
-        quantize_lane(3, keep.tile([P, P], U32, name="w_codes3", align_bytes=64), w_grouped3, halves)
-        multiply(bank23[:, 1, :], 3, dy_codes[:], dy_scales[:])
-
-        turned = gather_and_turn(DY2, LATE_VECTOR_SLOTS, picked_tile())
-        y23 = shared.tile([P, 2, PAIR.stop], F32, name="y23", offset=DY2 * WINDOW, align_bytes=64)
+        turned = sums.tile([P, 2, P], F32, name="bank01")
+        gather_shared_and_turn(windows[DY2][:], turned)
+        grouped = shared.tile([P, 2, LANES * P], BF16, name="w_grouped1", offset=DY2 * WINDOW, align_bytes=64)
+        group_lanes(*turned_lanes, grouped)
         rounded_pair = shared.tile(
             [P, PAIR.stop, LANES], BF16, name="rounded_pair", offset=DY2 * WINDOW + WINDOW // 2, align_bytes=64
         )
         nc.vector.tensor_copy(out=rounded_pair[:, :, 0:2], in_=y01[:].rearrange("p t r -> p r t"))
-        pair_tiles = [slice(j * P, (j + 1) * P) for j in range(2)]
+        quantize_lanes(1, keep.tile([P, 2 * P], U32, name="w_codes1", align_bytes=64), grouped)
+        bank23 = sums.tile([P, 2, PAIR.stop], F32, name="bank23")
+        for t in range(2):
+            multiply(bank23[:, t, :], 2 + t, dy_codes[:], dy_scales[:])
+        third_grouped = keep.tile([P, LANES * P], BF16, name="third_grouped", align_bytes=64)
+        nc.scalar.copy(**grouping(turned[:], third_grouped[:]))
+
+        turned = turn.tile([P, 2, P], F32, name="turned")
+        gather_shared_and_turn(windows[DY3][:], turned)
+        third_codes = shared.tile([P, P], U32, name="third_codes", offset=DY3 * WINDOW, align_bytes=64)
+        third_scales = keep.tile([P, P], U8, name="third_scales", align_bytes=64)
+        quantize_dy(third_codes, third_scales, third_grouped, whole)
+        y23 = shared.tile([P, 2, PAIR.stop], F32, name="y23", offset=DY3 * WINDOW + WINDOW // 2, align_bytes=64)
         for cols in pair_tiles:
             nc.scalar.copy(out=y23[:, :, cols], in_=bank23[:, :, cols])
         nc.sync.dma_start(out=out_rows[:, 2:4, PAIR], in_=y23[:])
         for cols in pair_tiles:
             nc.vector.tensor_copy(out=rounded_pair[:, cols, 2:4], in_=y23[:, :, cols].rearrange("p t r -> p r t"))
-        third_grouped = keep.tile([P, LANES * P], BF16, name="third_grouped", align_bytes=64)
-        group(turned[:], third_grouped[:])
-
-        turned = gather_and_turn(DY3, SLOTS // 2, picked_tile())
-        third_codes = shared.tile([P, P], U32, name="third_codes", offset=DY3 * WINDOW, align_bytes=64)
-        third_scales = keep.tile([P, P], U8, name="third_scales", align_bytes=64)
-        quantize_dy(third_codes, third_scales, third_grouped, whole)
-        pair_codes = shared.tile(
-            [P, PAIR.stop], U32, name="pair_codes", offset=DY3 * WINDOW + WINDOW // 2, align_bytes=64
-        )
-        quantize_result(PAIR, pair_codes[:], rounded_pair[:])
-        nc.sync.dma_start(out=out_words[:, PAIR], in_=pair_codes[:].bitcast(I32))
         third_low = sums.tile([P, 2, P], F32, name="third_low")
         third_high = sums.tile([P, 2, P], F32, name="third_high")
         for t in range(LANES):
             multiply((third_low, third_high)[t // 2][:, t % 2, :], t, third_codes[:], third_scales[:])
-        last_grouped = keep.tile([P, LANES * P], BF16, name="last_grouped", align_bytes=64)
+        last_grouped = shared.tile([P, LANES * P], BF16, name="last_grouped", offset=AFTER_WINDOWS, align_bytes=64)
         last_codes = keep.tile([P, P], U32, name="last_codes", align_bytes=64)
         last_scales = keep.tile([P, P], U8, name="last_scales", align_bytes=64)
         for rows in halves:
-            group(turned[:, :, rows], last_grouped[:, values(rows)])
+            nc.scalar.copy(**grouping(turned[:, :, rows], last_grouped[:, values(rows)]))
         quantize_dy(last_codes, last_scales, last_grouped, halves)
         last_banks = [sums.tile([P, P], F32, name=name) for name in ("low", "high", "bank01", "bank23")]
         for t in range(LANES):
             multiply(last_banks[t][:], t, last_codes[:], last_scales[:])
+        pair_codes = shared.tile([P, PAIR.stop], U32, name="pair_codes", offset=AFTER_WINDOWS, align_bytes=64)
+        quantize_result(PAIR, pair_codes[:], rounded_pair[:])
+        nc.sync.dma_start(out=out_words[:, PAIR], in_=pair_codes[:].bitcast(I32))
         y_third = keep.tile([P, LANES, P], F32, name="y_third", align_bytes=64)
         for lanes, bank in zip((slice(0, 2), slice(2, 4)), (third_low, third_high)):
             nc.scalar.copy(out=y_third[:, lanes, :], in_=bank[:])
@@ -233,7 +244,7 @@ def tile_attend_gmeprop_x_pl_kernel(tc, dy, wT, offs, out_0, out_1, out_2):
             )
         nc.sync.dma_start(out=out_words[:, PAIR.stop : R], in_=late_codes[:].bitcast(I32))
         for g in range(P // 32):
-            queue = nc.scalar if g % 2 == 0 else nc.sync
+            queue = nc.sync if g == 0 else nc.scalar
             queue.dma_start(
                 out=out_scales[4 * g : 4 * g + 4, :],
                 in_=y_scales[32 * g : 32 * g + 4, :].bitcast(I32),

from contextlib import ExitStack

import concourse.mybir as mybir
from concourse.masks import make_identity

F32 = mybir.dt.float32
BF16 = mybir.dt.bfloat16
I32 = mybir.dt.int32
U32 = mybir.dt.uint32
U16 = mybir.dt.uint16
U8 = mybir.dt.uint8
E4M3X4 = mybir.dt.float8_e4m3fn_x4
E5M2X4 = mybir.dt.float8_e5m2_x4
COPY = mybir.ActivationFunctionType.Copy

P = 128
LANES = 4
D = 512
R = 512
SLOTS = 512
UNITS = 2048
WINDOW = 4 * UNITS
PAIR = slice(0, 2 * P)
THIRD = slice(2 * P, 3 * P)
LAST = slice(3 * P, R)
DY2 = 0
DY3 = 1
LANES23 = 2
AFTER_WINDOWS = 4 * WINDOW

FLOPS = 2 * D * R * SLOTS


def tile_attend_gmeprop_x_pl_kernel(tc, dy, wT, offs, out_0, out_1, out_2):
    nc = tc.nc
    w_rows = wT.rearrange("(p t) k -> p t k", t=LANES)
    out_rows = out_0.rearrange("(p t) r -> p t r", t=LANES)
    out_words = out_1.rearrange("a p c l -> (a p) (c l)").bitcast(I32)
    out_scales = out_2.rearrange("a q c -> (a q) c").bitcast(I32)

    with ExitStack() as ctx:
        keep = ctx.enter_context(tc.tile_pool(name="keep", bufs=1))
        ring = ctx.enter_context(tc.tile_pool(name="ring", bufs=3))
        shared = ctx.enter_context(tc.tile_pool(name="shared", bufs=1))
        turn = ctx.enter_context(tc.psum_pool(name="turn", bufs=2))
        sums = ctx.enter_context(tc.psum_pool(name="sums", bufs=1))

        offsets = keep.tile([P, SLOTS // 16], U16, name="offsets")
        dy_pair = keep.tile([P, 2, UNITS], F32, name="dy_pair", align_bytes=64)
        nc.sync.dma_start(out=dy_pair[:], in_=dy[PAIR, :].rearrange("(p j) k -> p j k", j=2))
        nc.sync.dma_start(offsets[:], offs)
        w_pairs = [
            keep.tile([P, 2 * UNITS], F32, name="w_pair0", align_bytes=64),
            shared.tile([P, 2 * UNITS], F32, name="w_pair1", offset=LANES23 * WINDOW, align_bytes=64),
        ]
        for h in range(2):
            nc.sync.dma_start(
                out=w_pairs[h][:].rearrange("p (j k) -> p j k", j=2), in_=w_rows[:, 2 * h : 2 * h + 2, :]
            )
        windows = []
        for n, rows in enumerate((THIRD, LAST)):
            windows.append(shared.tile([P, UNITS], F32, name="window%d" % n, offset=n * WINDOW, align_bytes=64))
            nc.sync.dma_start(out=windows[n][:], in_=dy[rows, :])

        identity = keep.tile([P, P], F32, name="identity")
        make_identity(nc, identity[:])

        def picked_tile():
            return ring.tile([P, SLOTS], BF16, name="picked", align_bytes=64)

        def turn_as_listed(picked, turned):
            words = picked[:].bitcast(F32)
            for u in range(2):
                nc.tensor.transpose(turned[:, u, :], words[:, u : 2 * P : 2], identity[:])

        def gather_dealt_and_turn(window, turned):
            picked = picked_tile()
            nc.vector.tensor_copy(
                picked[:].rearrange("p (u s c) -> p s u c", u=2, c=2), window.indirect(offsets[:])
            )
            for u in range(2):
                nc.tensor.transpose(turned[:, u, :], picked[:].bitcast(F32)[:, u * P : (u + 1) * P], identity[:])

        def gather_shared_and_turn(window, turned):
            picked = picked_tile()
            half = SLOTS // 2
            nc.vector.tensor_copy(picked[:, 0:half], window.indirect(offsets[:, 0 : half // 16]))
            nc.scalar.activation(picked[:, half:SLOTS], window.indirect(offsets[:, half // 16 :]), COPY)
            turn_as_listed(picked, turned)

        def grouping(turned, grouped):
            return dict(
                out=grouped.bitcast(F32).rearrange("p (m u) -> p m u", u=2), in_=turned.rearrange("p u m -> p m u")
            )

        def values(cols):
            return slice(LANES * cols.start, LANES * cols.stop)

        def multiply(out, t, codes, scales):
            lane = slice(t % 2 * P, (t % 2 + 1) * P)
            nc.tensor.matmul_mx(
                out=out,
                lhsT=w_codes[t // 2][:, lane].bitcast(E4M3X4),
                lhsT_scale=w_scales[t // 2][:, lane],
                rhs=codes.bitcast(E5M2X4),
                rhs_scale=scales,
                start=True,
                stop=True,
            )

        def gather_lanes(h):
            turned_odd = turn.tile([P, 2, P], F32, name="turned")
            gather_dealt_and_turn(w_pairs[h][:, UNITS : 2 * UNITS], turned_odd)
            picked = picked_tile()
            nc.scalar.activation(picked[:], w_pairs[h][:].indirect(offsets[:]), COPY)
            turned_even = turn.tile([P, 2, P], F32, name="turned")
            turn_as_listed(picked, turned_even)
            return turned_even, turned_odd

        def group_lanes(turned_even, turned_odd, grouped):
            nc.vector.tensor_copy(**grouping(turned_odd[:], grouped[:, 1, :]))
            nc.scalar.copy(**grouping(turned_even[:], grouped[:, 0, :]))

        def quantize_lanes(h, codes, grouped):
            scales = keep.tile([P, 2 * P], U8, name="w_scales%d" % h, align_bytes=64)
            for j, cols in enumerate(pair_tiles):
                nc.vector.quantize_mx(out=codes[:, cols].bitcast(E4M3X4), scales=scales[:, cols], in_=grouped[:, j, :])
            w_codes.append(codes)
            w_scales.append(scales)

        def quantize_dy(codes, scales, grouped, pieces):
            for rows in pieces:
                nc.vector.quantize_mx(
                    out=codes[:, rows].bitcast(E5M2X4), scales=scales[:, rows], in_=grouped[:, values(rows)]
                )

        def round_result(rounded, y):
            nc.vector.tensor_copy(
                out=rounded.rearrange("p (c i) t -> p c t i", i=4), in_=y.rearrange("p t (c i) -> p c t i", i=4)
            )

        def quantize_result(cols, codes, rounded):
            nc.vector.quantize_mx(
                out=codes.bitcast(E4M3X4), scales=y_scales[:, cols], in_=rounded.rearrange("p r t -> p (r t)")
            )

        w_codes = []
        w_scales = []
        y_scales = keep.tile([P, R], U8, name="y_scales", align_bytes=64)
        whole = [slice(0, P)]
        halves = [slice(0, P // 2), slice(P // 2, P)]
        pair_tiles = [slice(j * P, (j + 1) * P) for j in range(2)]

        dy_grouped = keep.tile([P, LANES * PAIR.stop], BF16, name="dy_grouped", align_bytes=64)
        turned = turn.tile([P, 2, 2, P], F32, name="turned")
        for j in range(2):
            gather_dealt_and_turn(dy_pair[:, j, :], turned[:, j])
        nc.scalar.copy(
            out=dy_grouped[:].bitcast(F32).rearrange("p (m j u) -> p m j u", j=2, u=2),
            in_=turned[:].rearrange("p j u m -> p m j u"),
        )
        dy_codes = keep.tile([P, PAIR.stop], U32, name="dy_codes", align_bytes=64)
        dy_scales = keep.tile([P, PAIR.stop], U8, name="dy_scales", align_bytes=64)
        nc.vector.quantize_mx(out=dy_codes[:].bitcast(E5M2X4), scales=dy_scales[:], in_=dy_grouped[:])

        grouped = keep.tile([P, 2, LANES * P], BF16, name="w_grouped0", align_bytes=64)
        group_lanes(*gather_lanes(0), grouped)
        quantize_lanes(0, keep.tile([P, 2 * P], U32, name="w_codes0", align_bytes=64), grouped)
        bank01 = sums.tile([P, 2, PAIR.stop], F32, name="bank01")
        for t in range(2):
            multiply(bank01[:, t, :], t, dy_codes[:], dy_scales[:])

        turned_lanes = gather_lanes(1)
        y01 = shared.tile([P, 2, PAIR.stop], F32, name="y01", offset=LANES23 * WINDOW, align_bytes=64)
        nc.scalar.copy(out=y01[:], in_=bank01[:])
        nc.sync.dma_start(out=out_rows[:, 0:2, PAIR], in_=y01[:])
        turned = sums.tile([P, 2, P], F32, name="bank01")
        gather_shared_and_turn(windows[DY2][:], turned)
        grouped = shared.tile([P, 2, LANES * P], BF16, name="w_grouped1", offset=DY2 * WINDOW, align_bytes=64)
        group_lanes(*turned_lanes, grouped)
        rounded_pair = shared.tile(
            [P, PAIR.stop, LANES], BF16, name="rounded_pair", offset=DY2 * WINDOW + WINDOW // 2, align_bytes=64
        )
        nc.vector.tensor_copy(out=rounded_pair[:, :, 0:2], in_=y01[:].rearrange("p t r -> p r t"))
        quantize_lanes(1, keep.tile([P, 2 * P], U32, name="w_codes1", align_bytes=64), grouped)
        bank23 = sums.tile([P, 2, PAIR.stop], F32, name="bank23")
        for t in range(2):
            multiply(bank23[:, t, :], 2 + t, dy_codes[:], dy_scales[:])
        third_grouped = keep.tile([P, LANES * P], BF16, name="third_grouped", align_bytes=64)
        nc.scalar.copy(**grouping(turned[:], third_grouped[:]))

        turned = turn.tile([P, 2, P], F32, name="turned")
        gather_shared_and_turn(windows[DY3][:], turned)
        third_codes = shared.tile([P, P], U32, name="third_codes", offset=DY3 * WINDOW, align_bytes=64)
        third_scales = keep.tile([P, P], U8, name="third_scales", align_bytes=64)
        quantize_dy(third_codes, third_scales, third_grouped, whole)
        y23 = shared.tile([P, 2, PAIR.stop], F32, name="y23", offset=DY3 * WINDOW + WINDOW // 2, align_bytes=64)
        for cols in pair_tiles:
            nc.scalar.copy(out=y23[:, :, cols], in_=bank23[:, :, cols])
        nc.sync.dma_start(out=out_rows[:, 2:4, PAIR], in_=y23[:])
        for cols in pair_tiles:
            nc.vector.tensor_copy(out=rounded_pair[:, cols, 2:4], in_=y23[:, :, cols].rearrange("p t r -> p r t"))
        third_low = sums.tile([P, 2, P], F32, name="third_low")
        third_high = sums.tile([P, 2, P], F32, name="third_high")
        for t in range(LANES):
            multiply((third_low, third_high)[t // 2][:, t % 2, :], t, third_codes[:], third_scales[:])
        last_grouped = shared.tile([P, LANES * P], BF16, name="last_grouped", offset=AFTER_WINDOWS, align_bytes=64)
        last_codes = keep.tile([P, P], U32, name="last_codes", align_bytes=64)
        last_scales = keep.tile([P, P], U8, name="last_scales", align_bytes=64)
        for rows in halves:
            nc.scalar.copy(**grouping(turned[:, :, rows], last_grouped[:, values(rows)]))
        quantize_dy(last_codes, last_scales, last_grouped, halves)
        last_banks = [sums.tile([P, P], F32, name=name) for name in ("low", "high", "bank01", "bank23")]
        for t in range(LANES):
            multiply(last_banks[t][:], t, last_codes[:], last_scales[:])
        pair_codes = shared.tile([P, PAIR.stop], U32, name="pair_codes", offset=AFTER_WINDOWS, align_bytes=64)
        quantize_result(PAIR, pair_codes[:], rounded_pair[:])
        nc.sync.dma_start(out=out_words[:, PAIR], in_=pair_codes[:].bitcast(I32))
        y_third = keep.tile([P, LANES, P], F32, name="y_third", align_bytes=64)
        for lanes, bank in zip((slice(0, 2), slice(2, 4)), (third_low, third_high)):
            nc.scalar.copy(out=y_third[:, lanes, :], in_=bank[:])
            nc.sync.dma_start(out=out_rows[:, lanes, THIRD], in_=y_third[:, lanes, :])
        rounded_third = keep.tile([P, P, LANES], BF16, name="rounded_third", align_bytes=64)
        round_result(rounded_third[:], y_third[:])

        rounded_last = keep.tile([P, P, LANES], BF16, name="rounded_last", align_bytes=64)
        y_last = keep.tile([P, LANES, P], F32, name="y_last", align_bytes=64)
        late_codes = keep.tile([P, 2 * P], U32, name="late_codes", align_bytes=64)
        for t in range(2):
            nc.scalar.copy(out=y_last[:, t, :], in_=last_banks[t][:])
        nc.sync.dma_start(out=out_rows[:, 0:2, LAST], in_=y_last[:, 0:2, :])
        quantize_result(THIRD, late_codes[:, 0:P], rounded_third[:])
        nc.scalar.copy(out=y_last[:, 2, :], in_=last_banks[2][:])
        for cols in halves:
            nc.scalar.copy(out=y_last[:, 3, cols], in_=last_banks[3][:, cols])
        nc.sync.dma_start(out=out_rows[:, 2:4, LAST], in_=y_last[:, 2:4, :])
        for cols in halves:
            round_result(rounded_last[:, cols, :], y_last[:, :, cols])
        for cols in halves:
            quantize_result(
                slice(LAST.start + cols.start, LAST.start + cols.stop),
                late_codes[:, P + cols.start : P + cols.stop],
                rounded_last[:, cols, :],
            )
        nc.sync.dma_start(out=out_words[:, PAIR.stop : R], in_=late_codes[:].bitcast(I32))
        for g in range(P // 32):
            queue = nc.sync if g == 0 else nc.scalar
            queue.dma_start(
                out=out_scales[4 * g : 4 * g + 4, :],
                in_=y_scales[32 * g : 32 * g + 4, :].bitcast(I32),
            )
